import numpy as np
import ml_dtypes


def mxq(x, axis, fmt="e4m3"):
    dtype, down = {"e4m3": (ml_dtypes.float8_e4m3fn, 7), "e5m2": (ml_dtypes.float8_e5m2, 14)}[fmt]
    v = np.moveaxis(np.asarray(x, np.float32).astype(ml_dtypes.bfloat16).astype(np.float64), axis, -1)
    blocks = v.reshape(v.shape[:-1] + (-1, 32))
    amax = np.abs(blocks).max(-1, keepdims=True)
    byte = np.maximum(np.where(amax > 0, np.frexp(amax)[1] - 1 + 127, 0) - down, 1)
    scale = np.exp2(byte - 127.0)
    codes = (blocks / scale).astype(np.float32).astype(dtype).astype(np.float64)
    return np.moveaxis((codes * scale).reshape(v.shape), -1, axis)


WIDE = False


def mx_kscale(k):
    if not WIDE:
        return np.ones(k)
    levels = np.array([10, -10, 5, -5, 0])
    if k % 512:
        return np.exp2(np.random.permutation(np.resize(levels, k // 32))).repeat(32)
    a = np.empty((k // 512, 16))
    for p in range(k // 512):
        a[p, :8] = np.random.permutation(np.resize(levels, 8))
        for g in range(8):
            far = levels[np.abs(levels - a[p, g]) >= 10]
            a[p, g + 8] = far[np.random.randint(len(far))]
    return np.exp2(a.ravel()).repeat(32)


def f64(x):
    return np.asarray(x).astype(np.float64)


def striped(idx):
    return np.tile(np.asarray(idx).reshape(-1, 16).T, (8, 1)).astype(np.uint16)


def unstriped(offs):
    return offs[:16].T.reshape(-1).astype(np.int64)


E2M1 = np.array([0.0, 0.5, 1.0, 1.5, 2.0, 3.0, 4.0, 6.0, -0.0, -0.5, -1.0, -1.5, -2.0, -3.0, -4.0, -6.0])


def pack_weight(w, fmt):
    k, n = w.shape
    w = f64(np.asarray(w, np.float32).astype(ml_dtypes.bfloat16)).reshape(k // 32, 32, n)
    amax = np.abs(w).max(1)
    if fmt == "e4m3":
        byte = np.frexp(amax)[1] - 1 + 127 - 7
    else:
        mant, ex = np.frexp(amax / 6.0)
        byte = np.where(mant > 0.5, ex, ex - 1) + 127
    byte = np.clip(np.where(amax > 0, byte, 1), 1, 254)
    scaled = (w * np.exp2(127.0 - byte)[:, None, :]).reshape(k, n).astype(np.float32)
    by_word = np.ascontiguousarray(scaled.reshape(k // 512, 128, 4, n).transpose(0, 1, 3, 2))
    if fmt == "e4m3":
        words = by_word.astype(ml_dtypes.float8_e4m3fn).view(np.uint8)
    else:
        c = by_word.astype(ml_dtypes.float4_e2m1fn).view(np.uint8) & 0xF
        words = (c[..., 0::2] | (c[..., 1::2] << 4)).reshape(k // 512, 128, 2 * n)
    return np.ascontiguousarray(words), np.ascontiguousarray(byte.astype(np.uint8).reshape(k // 512, 16, n))


def unpack_weight(words, scales, fmt):
    g, _, n = scales.shape
    words = np.ascontiguousarray(words).reshape(g, 128, n, -1)
    if fmt == "e4m3":
        vals = words.view(ml_dtypes.float8_e4m3fn).astype(np.float64)
    else:
        nib = np.empty((g, 128, n, 4), np.uint8)
        nib[..., 0::2] = words & 0xF
        nib[..., 1::2] = words >> 4
        vals = E2M1[nib]
    vals = vals * np.repeat(np.exp2(scales.astype(np.float64) - 127.0), 8, axis=1)[..., None]
    return vals.transpose(0, 1, 3, 2).reshape(g * 512, n)


B, N, T, D, DV, NQ = 2, 1024, 4096, 1024, 128, 128
PAGE = 512


def setup_inputs():
    n = np.random.standard_normal
    pages = np.random.permutation(T // PAGE)[:B * N // PAGE]
    idx = (pages[:, None] * PAGE + np.arange(PAGE)[None, :]).reshape(-1)
    s = mx_kscale(D)[:, None]
    u = np.ones(T)
    u[idx] = mx_kscale(B * N)
    r = np.random.uniform(0.5, 2.0, T)
    qp = [pack_weight(x, "e4m3") for x in n((B, D, NQ)) * s * (1.00 / np.sqrt(D))]
    k = n((D, T)) / s
    v = n((DV, T)) / (u * r)
    kp = pack_weight(k, "e2m1")
    vp = pack_weight(v.T, "e4m3")
    return {
        "q_words": np.stack([x[0] for x in qp]),
        "q_scales": np.stack([x[1] for x in qp]),
        "k_words": np.ascontiguousarray(kp[0].reshape(D // 1024, 2, 128, T, 2).transpose(0, 2, 3, 1, 4)).reshape(D // 1024, 128, T, 4),
        "k_scales": kp[1],
        "v_words": vp[0],
        "v_scales": vp[1],
        "vs": np.tile(u * r, (128, 1)).astype(np.float32),
        "offs": striped(idx),
        "voffs": striped((pages[:, None] * DV + np.arange(DV)[None, :]).reshape(-1)),
    }


def reference(q_words, q_scales, k_words, k_scales, v_words, v_scales, vs, offs, voffs):
    idx = unstriped(offs)
    k = unpack_weight(k_words.reshape(D // 1024, 128, T, 2, 2).transpose(0, 3, 1, 2, 4).reshape(D // 512, 128, 2 * T), k_scales, "e2m1")
    v = unpack_weight(v_words, v_scales, "e4m3")
    v = v.reshape(T // 512, 512, DV)[unstriped(voffs)[::DV] // DV].reshape(B, N, DV)
    pick = lambda x: x[:, idx].reshape(x.shape[0], B, N).transpose(1, 0, 2)
    q = np.stack([unpack_weight(q_words[b], q_scales[b], "e4m3") for b in range(B)])
    score = q.transpose(0, 2, 1) @ pick(k)
    p = 1.0 / (1.0 + np.exp(-score))
    w = p * pick(f64(vs))[:, :1, :]
    y = mxq(w, 2, "e4m3") @ v
    y = y / 16.0
    return y

@@ -1,0 +1,199 @@
+from contextlib import ExitStack
+
+import concourse.mybir as mybir
+from concourse.masks import make_identity
+
+B, N, T, D, DV, NQ = 2, 1024, 4096, 1024, 128, 128
+P = 128
+PAGE = 512
+PACK = 4
+PAGES = B * N // PAGE
+POOL_PAGES = T // PAGE
+PASSES = D // 512
+FLOPS = 2 * B * NQ * N * (D + DV)
+
+F32 = mybir.dt.float32
+BF16 = mybir.dt.bfloat16
+I32 = mybir.dt.int32
+U32 = mybir.dt.uint32
+U16 = mybir.dt.uint16
+U8 = mybir.dt.uint8
+FP8X4 = mybir.dt.float8_e4m3fn_x4
+FP4X4 = mybir.dt.float4_e2m1fn_x4
+ACT = mybir.ActivationFunctionType
+MULT = mybir.AluOpType.mult
+
+
+def tile_attend_pkv4q_sigm_kernel(
+    tc, q_words, q_scales, k_words, k_scales, v_words, v_scales, vs, offs, voffs, out
+):
+    nc = tc.nc
+    with ExitStack() as ctx:
+        keep = ctx.enter_context(tc.tile_pool(name="keep", bufs=1))
+        reuse = ctx.enter_context(tc.tile_pool(name="reuse", bufs=1))
+        psum = ctx.enter_context(tc.psum_pool(name="psum", bufs=1))
+
+        offs_sb = keep.tile([P, B * N // 16], U16, name="offs_sb")
+        voffs_sb = keep.tile([P, PAGES * DV // 16], U16, name="voffs_sb")
+        kw_pool = keep.tile([P, T], I32, name="kw_pool", align_bytes=64)
+        ks_pool = keep.tile([P, T], U8, name="ks_pool", align_bytes=64)
+        vw_pool = keep.tile([P, POOL_PAGES * DV], I32, name="vw_pool", align_bytes=64)
+        vsc_pool = keep.tile([P, POOL_PAGES * DV], U8, name="vsc_pool", align_bytes=64)
+        vs_pool = reuse.tile([P, T], F32, name="vs_pool", align_bytes=64, offset=0)
+        qw = keep.tile([P, B * PASSES * NQ], I32, name="qw", align_bytes=64)
+        qsc = keep.tile([P, B * PASSES * NQ], U8, name="qsc", align_bytes=64)
+        ks_got = keep.tile([P, B * N], U8, name="ks_got", align_bytes=64)
+        ks_pass1 = keep.tile([P, B * N], U8, name="ks_pass1", align_bytes=64)
+        vs_got = keep.tile([P, B * N], F32, name="vs_got", align_bytes=64)
+        ident = keep.tile([P, P], F32, name="ident")
+        warm_in = keep.tile([P, 8], F32, name="warm_in")
+        warm = keep.tile([P, 8], F32, name="warm")
+
+        nc.vector.memset(ks_pool[:].bitcast(I32), 0)
+        nc.vector.memset(qsc[:].bitcast(I32), 0)
+        nc.vector.memset(warm_in[:], 0.0)
+        nc.vector.memset(vsc_pool[:].bitcast(I32), 0)
+        nc.vector.memset(ks_pass1[:].bitcast(I32), 0)
+        nc.vector.memset(vs_pool[:].bitcast(I32), 0)
+        make_identity(nc, ident[:])
+
+        nc.sync.dma_start(offs_sb[:], offs)
+        nc.sync.dma_start(voffs_sb[:], voffs)
+        nc.scalar.dma_start(out=ks_pool[4:P:8, :].bitcast(I32), in_=k_scales[1].bitcast(I32))
+        for quad in range(4):
+            nc.scalar.dma_start(
+                out=ks_pool[32 * quad : 32 * quad + 4, :].bitcast(I32),
+                in_=k_scales[0, 4 * quad : 4 * quad + 4, :].bitcast(I32),
+            )
+        nc.scalar.activation(out=warm[:], in_=warm_in[:], func=ACT.Sigmoid)
+        nc.sync.dma_start(
+            out=qw[:].rearrange("g (c q) -> g c q", q=NQ),
+            in_=q_words.rearrange("b o g q r -> g (b o) (q r)").bitcast(I32),
+        )
+        nc.sync.dma_start(out=kw_pool[:], in_=k_words[0].rearrange("g t r -> g (t r)").bitcast(I32))
+        nc.sync.dma_start(
+            out=vw_pool[:].rearrange("g (u e) -> g u e", e=DV),
+            in_=v_words.rearrange("u g e r -> g u (e r)").bitcast(I32),
+        )
+        q_rows = q_scales.rearrange("b o f q -> f (b o) q").bitcast(I32)
+        v_rows = v_scales.rearrange("u f e -> f u e").bitcast(I32)
+        for quad in range(4):
+            nc.gpsimd.dma_start(
+                out=qsc[32 * quad : 32 * quad + 4, :].bitcast(I32).rearrange("f (c q) -> f c q", c=B * PASSES),
+                in_=q_rows[4 * quad : 4 * quad + 4],
+            )
+        for quad in range(4):
+            nc.gpsimd.dma_start(
+                out=vsc_pool[32 * quad : 32 * quad + 4, :].bitcast(I32).rearrange("f (u e) -> f u e", u=POOL_PAGES),
+                in_=v_rows[4 * quad : 4 * quad + 4],
+            )
+        nc.scalar.dma_start(out=vs_pool[0:1, :], in_=vs[0:1, :])
+
+        nc.vector.tensor_copy(ks_got[:], ks_pool[:].indirect(offs_sb[:]))
+        for quad in range(4):
+            nc.sync.dma_start(
+                out=ks_pass1[32 * quad : 32 * quad + 4, :].bitcast(I32),
+                in_=ks_got[32 * quad + 4 : 32 * quad + 32 : 8, :].bitcast(I32),
+            )
+        nc.vector.tensor_copy(vs_got[:], vs_pool[:].indirect(offs_sb[:]))
+        vs_slot = []
+        for e in range(PAGES):
+            col = keep.tile([P, PACK], F32, name=f"vs_slot{e}")
+            nc.sync.dma_start(out=col[:], in_=vs_got[0:1, e * PAGE : (e + 1) * PAGE])
+            vs_slot.append(col)
+        ks_plane = [ks_got, ks_pass1]
+
+        kw_got = [
+            reuse.tile([P, PAGE], U32, name=f"kw_got{e}", align_bytes=64, offset=(e % 2) * 4 * PAGE)
+            for e in range(PAGES)
+        ]
+        vw_got = reuse.tile([P, PAGES * DV], U32, name="vw_got", align_bytes=64, offset=0)
+        vsc_got = reuse.tile([P, PAGES * DV], U8, name="vsc_got", align_bytes=64, offset=4 * PAGE)
+        kw_part = [keep.tile([P, PASSES, PAGE], U16, name=f"kw_part{e}", align_bytes=64) for e in range(PAGES)]
+        p_sb = [keep.tile([P, PACK, P], F32, name=f"p_sb{e}", align_bytes=64) for e in range(PAGES)]
+        w_bf = [keep.tile([P, NQ, PACK], BF16, name=f"w_bf{e}", align_bytes=64) for e in range(PAGES)]
+        w_codes = [keep.tile([P, NQ], U32, name=f"w_codes{e}", align_bytes=64) for e in range(PAGES)]
+        w_scale = [keep.tile([P, NQ], U8, name=f"w_scale{e}", align_bytes=64) for e in range(PAGES)]
+        score = [psum.tile([P, PAGE], F32, name=f"score{e}", tag=f"score{e % 2}") for e in range(2)]
+        p_turn = [psum.tile([P, PACK, P], F32, name=f"p_turn{e}") for e in range(PAGES)]
+        y_ps = [psum.tile([P, DV], F32, name=f"y_ps{b}") for b in range(B)]
+
+        def gather_keys(e):
+            cols = slice(e * PAGE // 16, (e + 1) * PAGE // 16)
+            nc.vector.tensor_copy(kw_got[e][:], kw_pool[:].bitcast(U32).indirect(offs_sb[:, cols]))
+
+        def part_keys(e):
+            nc.vector.tensor_copy(kw_part[e][:], kw_got[e][:].bitcast(U16).rearrange("g (n o) -> g o n", o=PASSES))
+
+        def scores(e):
+            b = e * PAGE // N
+            for o in range(PASSES):
+                q_cols = slice((b * PASSES + o) * NQ, (b * PASSES + o + 1) * NQ)
+                nc.tensor.matmul_mx(
+                    out=score[e % 2][:],
+                    lhsT=qw[:, q_cols].bitcast(FP8X4),
+                    lhsT_scale=qsc[:, q_cols],
+                    rhs=kw_part[e][:, o, :].bitcast(FP4X4),
+                    rhs_scale=ks_plane[o][:, e * PAGE : (e + 1) * PAGE],
+                    start=(o == 0),
+                    stop=(o == PASSES - 1),
+                )
+            nc.scalar.activation(
+                out=p_sb[e][:], in_=score[e % 2][:].rearrange("q (m t) -> q t m", t=PACK), func=ACT.Sigmoid
+            )
+
+        def turn(e):
+            for t in range(PACK):
+                nc.tensor.transpose(p_turn[e][:, t, :], p_sb[e][:, t, :], ident[:])
+
+        def weigh(e):
+            nc.vector.tensor_tensor(
+                w_bf[e][:],
+                p_turn[e][:].rearrange("m t q -> m q t"),
+                vs_slot[e][:].unsqueeze(1).to_broadcast([P, NQ, PACK]),
+                MULT,
+            )
+
+        def quantise(e):
+            nc.vector.quantize_mx(
+                out=w_codes[e][:].bitcast(FP8X4), scales=w_scale[e][:], in_=w_bf[e][:].rearrange("m q t -> m (q t)")
+            )
+
+        def mix(e):
+            b, first = divmod(e, N // PAGE)
+            v_cols = slice(e * DV, (e + 1) * DV)
+            nc.tensor.matmul_mx(
+                out=y_ps[b][:],
+                lhsT=w_codes[e][:].bitcast(FP8X4),
+                lhsT_scale=w_scale[e][:],
+                rhs=vw_got[:, v_cols].bitcast(FP8X4),
+                rhs_scale=vsc_got[:, v_cols],
+                start=(first == 0),
+                stop=(first == N // PAGE - 1),
+            )
+
+        def store(b):
+            y_sb = keep.tile([P, DV], F32, name=f"y_sb{b}")
+            nc.scalar.activation(out=y_sb[:], in_=y_ps[b][:], func=ACT.Copy, scale=1.0 / 16.0)
+            nc.sync.dma_start(out=out[b], in_=y_sb[:])
+
+        for pair in range(0, PAGES, 2):
+            gather_keys(pair)
+            gather_keys(pair + 1)
+            part_keys(pair)
+            part_keys(pair + 1)
+        nc.vector.tensor_copy(vw_got[:], vw_pool[:].bitcast(U32).indirect(voffs_sb[:]))
+        nc.vector.tensor_copy(vsc_got[:], vsc_pool[:].indirect(voffs_sb[:]))
+        for e in range(PAGES):
+            scores(e)
+            if e > 0:
+                turn(e - 1)
+        turn(PAGES - 1)
+        weigh(0)
+        for e in range(PAGES):
+            if e + 1 < PAGES:
+                weigh(e + 1)
+            quantise(e)
+            mix(e)
+            if e % 2 == 1:
+                store(e // 2)

@@ -10,6 +10,8 @@ PACK = 4
 PAGES = B * N // PAGE
 POOL_PAGES = T // PAGE
 PASSES = D // 512
+SLOT_BYTES = 4 * PAGE
+POOL_AT = 2 * SLOT_BYTES
 FLOPS = 2 * B * NQ * N * (D + DV)
 
 F32 = mybir.dt.float32
@@ -36,29 +38,35 @@ def tile_attend_pkv4q_sigm_kernel(
         offs_sb = keep.tile([P, B * N // 16], U16, name="offs_sb")
         voffs_sb = keep.tile([P, PAGES * DV // 16], U16, name="voffs_sb")
         kw_pool = keep.tile([P, T], I32, name="kw_pool", align_bytes=64)
-        ks_pool = keep.tile([P, T], U8, name="ks_pool", align_bytes=64)
+        ks_pool = reuse.tile([P, T], U8, name="ks_pool", align_bytes=64, offset=SLOT_BYTES // 2)
         vw_pool = keep.tile([P, POOL_PAGES * DV], I32, name="vw_pool", align_bytes=64)
         vsc_pool = keep.tile([P, POOL_PAGES * DV], U8, name="vsc_pool", align_bytes=64)
-        vs_pool = reuse.tile([P, T], F32, name="vs_pool", align_bytes=64, offset=0)
         qw = keep.tile([P, B * PASSES * NQ], I32, name="qw", align_bytes=64)
         qsc = keep.tile([P, B * PASSES * NQ], U8, name="qsc", align_bytes=64)
         ks_got = keep.tile([P, B * N], U8, name="ks_got", align_bytes=64)
         ks_pass1 = keep.tile([P, B * N], U8, name="ks_pass1", align_bytes=64)
-        vs_got = keep.tile([P, B * N], F32, name="vs_got", align_bytes=64)
+        vw_got = keep.tile([P, PAGES * DV], U32, name="vw_got", align_bytes=64)
         ident = keep.tile([P, P], F32, name="ident")
         warm_in = keep.tile([P, 8], F32, name="warm_in")
         warm = keep.tile([P, 8], F32, name="warm")
 
         nc.vector.memset(ks_pool[:].bitcast(I32), 0)
-        nc.vector.memset(qsc[:].bitcast(I32), 0)
+        nc.gpsimd.memset(qsc[:].bitcast(I32), 0)
         nc.vector.memset(warm_in[:], 0.0)
         nc.vector.memset(vsc_pool[:].bitcast(I32), 0)
         nc.vector.memset(ks_pass1[:].bitcast(I32), 0)
-        nc.vector.memset(vs_pool[:].bitcast(I32), 0)
-        make_identity(nc, ident[:])
 
-        nc.sync.dma_start(offs_sb[:], offs)
         nc.sync.dma_start(voffs_sb[:], voffs)
+        nc.sync.dma_start(
+            out=vw_pool[:].rearrange("g (u e) -> g u e", e=DV),
+            in_=v_words.rearrange("u g e r -> g u (e r)").bitcast(I32),
+        )
+        nc.sync.dma_start(offs_sb[:], offs)
+        nc.sync.dma_start(
+            out=qw[:].rearrange("g (c q) -> g c q", q=NQ),
+            in_=q_words.rearrange("b o g q r -> g (b o) (q r)").bitcast(I32),
+        )
+        nc.sync.dma_start(out=kw_pool[:], in_=k_words[0].rearrange("g t r -> g (t r)").bitcast(I32))
         nc.scalar.dma_start(out=ks_pool[4:P:8, :].bitcast(I32), in_=k_scales[1].bitcast(I32))
         for quad in range(4):
             nc.scalar.dma_start(
@@ -66,15 +74,6 @@ def tile_attend_pkv4q_sigm_kernel(
                 in_=k_scales[0, 4 * quad : 4 * quad + 4, :].bitcast(I32),
             )
         nc.scalar.activation(out=warm[:], in_=warm_in[:], func=ACT.Sigmoid)
-        nc.sync.dma_start(
-            out=qw[:].rearrange("g (c q) -> g c q", q=NQ),
-            in_=q_words.rearrange("b o g q r -> g (b o) (q r)").bitcast(I32),
-        )
-        nc.sync.dma_start(out=kw_pool[:], in_=k_words[0].rearrange("g t r -> g (t r)").bitcast(I32))
-        nc.sync.dma_start(
-            out=vw_pool[:].rearrange("g (u e) -> g u e", e=DV),
-            in_=v_words.rearrange("u g e r -> g u (e r)").bitcast(I32),
-        )
         q_rows = q_scales.rearrange("b o f q -> f (b o) q").bitcast(I32)
         v_rows = v_scales.rearrange("u f e -> f u e").bitcast(I32)
         for quad in range(4):
@@ -82,40 +81,43 @@ def tile_attend_pkv4q_sigm_kernel(
                 out=qsc[32 * quad : 32 * quad + 4, :].bitcast(I32).rearrange("f (c q) -> f c q", c=B * PASSES),
                 in_=q_rows[4 * quad : 4 * quad + 4],
             )
+        make_identity(nc, ident[:])
         for quad in range(4):
-            nc.gpsimd.dma_start(
+            nc.scalar.dma_start(
                 out=vsc_pool[32 * quad : 32 * quad + 4, :].bitcast(I32).rearrange("f (u e) -> f u e", u=POOL_PAGES),
                 in_=v_rows[4 * quad : 4 * quad + 4],
             )
-        nc.scalar.dma_start(out=vs_pool[0:1, :], in_=vs[0:1, :])
 
+        nc.vector.tensor_copy(vw_got[:], vw_pool[:].bitcast(U32).indirect(voffs_sb[:]))
         nc.vector.tensor_copy(ks_got[:], ks_pool[:].indirect(offs_sb[:]))
         for quad in range(4):
             nc.sync.dma_start(
                 out=ks_pass1[32 * quad : 32 * quad + 4, :].bitcast(I32),
                 in_=ks_got[32 * quad + 4 : 32 * quad + 32 : 8, :].bitcast(I32),
             )
-        nc.vector.tensor_copy(vs_got[:], vs_pool[:].indirect(offs_sb[:]))
-        vs_slot = []
-        for e in range(PAGES):
-            col = keep.tile([P, PACK], F32, name=f"vs_slot{e}")
-            nc.sync.dma_start(out=col[:], in_=vs_got[0:1, e * PAGE : (e + 1) * PAGE])
-            vs_slot.append(col)
+        vs_pool = reuse.tile([P, T], F32, name="vs_pool", align_bytes=64, offset=POOL_AT)
+        nc.sync.dma_start(out=vs_pool[:], in_=vs)
         ks_plane = [ks_got, ks_pass1]
 
         kw_got = [
-            reuse.tile([P, PAGE], U32, name=f"kw_got{e}", align_bytes=64, offset=(e % 2) * 4 * PAGE)
+            reuse.tile([P, PAGE], U32, name=f"kw_got{e}", align_bytes=64, offset=(e % 2) * SLOT_BYTES)
             for e in range(PAGES)
         ]
-        vw_got = reuse.tile([P, PAGES * DV], U32, name="vw_got", align_bytes=64, offset=0)
-        vsc_got = reuse.tile([P, PAGES * DV], U8, name="vsc_got", align_bytes=64, offset=4 * PAGE)
+        vsc_got = reuse.tile([P, PAGES * DV], U8, name="vsc_got", align_bytes=64, offset=POOL_AT)
+        w_f32 = [
+            reuse.tile([P, PAGE], F32, name=f"w_f32{e}", align_bytes=64, offset=e * SLOT_BYTES)
+            if e < 2
+            else keep.tile([P, PAGE], F32, name=f"w_f32{e}", align_bytes=64)
+            for e in range(PAGES)
+        ]
+        w_pair = [keep.tile([P, 2, P, 2], BF16, name=f"w_pair{e}", align_bytes=64) for e in range(PAGES)]
         kw_part = [keep.tile([P, PASSES, PAGE], U16, name=f"kw_part{e}", align_bytes=64) for e in range(PAGES)]
-        p_sb = [keep.tile([P, PACK, P], F32, name=f"p_sb{e}", align_bytes=64) for e in range(PAGES)]
+        p_sb = [keep.tile([P, PAGE], F32, name=f"p_sb{e}", align_bytes=64) for e in range(PAGES)]
         w_bf = [keep.tile([P, NQ, PACK], BF16, name=f"w_bf{e}", align_bytes=64) for e in range(PAGES)]
         w_codes = [keep.tile([P, NQ], U32, name=f"w_codes{e}", align_bytes=64) for e in range(PAGES)]
         w_scale = [keep.tile([P, NQ], U8, name=f"w_scale{e}", align_bytes=64) for e in range(PAGES)]
         score = [psum.tile([P, PAGE], F32, name=f"score{e}", tag=f"score{e % 2}") for e in range(2)]
-        p_turn = [psum.tile([P, PACK, P], F32, name=f"p_turn{e}") for e in range(PAGES)]
+        w_turn = [psum.tile([P, 2, P], F32, name=f"w_turn{e}") for e in range(PAGES)]
         y_ps = [psum.tile([P, DV], F32, name=f"y_ps{b}") for b in range(B)]
 
         def gather_keys(e):
@@ -138,20 +140,20 @@ def tile_attend_pkv4q_sigm_kernel(
                     start=(o == 0),
                     stop=(o == PASSES - 1),
                 )
-            nc.scalar.activation(
-                out=p_sb[e][:], in_=score[e % 2][:].rearrange("q (m t) -> q t m", t=PACK), func=ACT.Sigmoid
-            )
-
-        def turn(e):
-            for t in range(PACK):
-                nc.tensor.transpose(p_turn[e][:, t, :], p_sb[e][:, t, :], ident[:])
+            nc.scalar.activation(out=p_sb[e][:], in_=score[e % 2][:], func=ACT.Sigmoid)
 
         def weigh(e):
-            nc.vector.tensor_tensor(
-                w_bf[e][:],
-                p_turn[e][:].rearrange("m t q -> m q t"),
-                vs_slot[e][:].unsqueeze(1).to_broadcast([P, NQ, PACK]),
-                MULT,
+            cols = slice(e * PAGE // 16, (e + 1) * PAGE // 16)
+            nc.vector.tensor_tensor(w_f32[e][:], vs_pool[:].indirect(offs_sb[:, cols]), p_sb[e][:], MULT)
+
+        def turn(e):
+            nc.scalar.copy(out=w_pair[e][:], in_=w_f32[e][:].rearrange("q (m u r) -> q u m r", u=2, r=2))
+            words = w_pair[e][:].rearrange("q u m r -> q (u m r)").bitcast(F32)
+            for u in range(2):
+                nc.tensor.transpose(w_turn[e][:, u, :], words[:, u * P : (u + 1) * P], ident[:])
+            nc.scalar.copy(
+                out=w_bf[e][:].rearrange("m q t -> m (q t)").bitcast(F32).rearrange("m (q u) -> m q u", u=2),
+                in_=w_turn[e][:].rearrange("m u q -> m q u"),
             )
 
         def quantise(e):
@@ -182,17 +184,13 @@ def tile_attend_pkv4q_sigm_kernel(
             gather_keys(pair + 1)
             part_keys(pair)
             part_keys(pair + 1)
-        nc.vector.tensor_copy(vw_got[:], vw_pool[:].bitcast(U32).indirect(voffs_sb[:]))
-        nc.vector.tensor_copy(vsc_got[:], vsc_pool[:].indirect(voffs_sb[:]))
         for e in range(PAGES):
             scores(e)
-            if e > 0:
-                turn(e - 1)
-        turn(PAGES - 1)
-        weigh(0)
         for e in range(PAGES):
-            if e + 1 < PAGES:
-                weigh(e + 1)
+            weigh(e)
+            turn(e)
+        nc.vector.tensor_copy(vsc_got[:], vsc_pool[:].indirect(voffs_sb[:]))
+        for e in range(PAGES):
             quantise(e)
             mix(e)
             if e % 2 == 1:

@@ -12,6 +12,7 @@ POOL_PAGES = T // PAGE
 PASSES = D // 512
 SLOT_BYTES = 4 * PAGE
 POOL_AT = 2 * SLOT_BYTES
+FOLD = T // P
 FLOPS = 2 * B * NQ * N * (D + DV)
 
 F32 = mybir.dt.float32
@@ -38,42 +39,41 @@ def tile_attend_pkv4q_sigm_kernel(
         offs_sb = keep.tile([P, B * N // 16], U16, name="offs_sb")
         voffs_sb = keep.tile([P, PAGES * DV // 16], U16, name="voffs_sb")
         kw_pool = keep.tile([P, T], I32, name="kw_pool", align_bytes=64)
-        ks_pool = reuse.tile([P, T], U8, name="ks_pool", align_bytes=64, offset=SLOT_BYTES // 2)
+        ks_pool = reuse.tile([P, T], U8, name="ks_pool", align_bytes=64, offset=0)
+        vs_pool = reuse.tile([P, T], F32, name="vs_pool", align_bytes=64, offset=POOL_AT)
         vw_pool = keep.tile([P, POOL_PAGES * DV], I32, name="vw_pool", align_bytes=64)
         vsc_pool = keep.tile([P, POOL_PAGES * DV], U8, name="vsc_pool", align_bytes=64)
         qw = keep.tile([P, B * PASSES * NQ], I32, name="qw", align_bytes=64)
         qsc = keep.tile([P, B * PASSES * NQ], U8, name="qsc", align_bytes=64)
         ks_got = keep.tile([P, B * N], U8, name="ks_got", align_bytes=64)
-        ks_pass1 = keep.tile([P, B * N], U8, name="ks_pass1", align_bytes=64)
-        vw_got = keep.tile([P, PAGES * DV], U32, name="vw_got", align_bytes=64)
+        ks_plane = keep.tile([P, PASSES, B * N], U8, name="ks_plane", align_bytes=64)
+        vs_fold = keep.tile([P, FOLD], F32, name="vs_fold")
         ident = keep.tile([P, P], F32, name="ident")
         warm_in = keep.tile([P, 8], F32, name="warm_in")
         warm = keep.tile([P, 8], F32, name="warm")
+        nc.gpsimd.memset(warm_in[:], 0.0)
+        nc.scalar.activation(out=warm[:], in_=warm_in[:], func=ACT.Sigmoid)
 
-        nc.vector.memset(ks_pool[:].bitcast(I32), 0)
-        nc.gpsimd.memset(qsc[:].bitcast(I32), 0)
-        nc.vector.memset(warm_in[:], 0.0)
-        nc.vector.memset(vsc_pool[:].bitcast(I32), 0)
-        nc.vector.memset(ks_pass1[:].bitcast(I32), 0)
-
+        nc.sync.dma_start(out=ks_pool[0:32, :].bitcast(I32), in_=k_scales.rearrange("o f t -> (o f) t").bitcast(I32))
+        nc.sync.dma_start(offs_sb[:], offs)
+        nc.sync.dma_start(out=vs_fold[:], in_=vs[0].rearrange("(n m) -> n m", m=FOLD))
+        nc.sync.dma_start(out=kw_pool[:], in_=k_words[0].rearrange("g t r -> g (t r)").bitcast(I32))
+        nc.sync.dma_start(
+            out=qw[:].rearrange("g (c q) -> g c q", q=NQ),
+            in_=q_words.rearrange("b o g q r -> g (b o) (q r)").bitcast(I32),
+        )
         nc.sync.dma_start(voffs_sb[:], voffs)
         nc.sync.dma_start(
             out=vw_pool[:].rearrange("g (u e) -> g u e", e=DV),
             in_=v_words.rearrange("u g e r -> g u (e r)").bitcast(I32),
         )
-        nc.sync.dma_start(offs_sb[:], offs)
-        nc.sync.dma_start(
-            out=qw[:].rearrange("g (c q) -> g c q", q=NQ),
-            in_=q_words.rearrange("b o g q r -> g (b o) (q r)").bitcast(I32),
-        )
-        nc.sync.dma_start(out=kw_pool[:], in_=k_words[0].rearrange("g t r -> g (t r)").bitcast(I32))
-        nc.scalar.dma_start(out=ks_pool[4:P:8, :].bitcast(I32), in_=k_scales[1].bitcast(I32))
-        for quad in range(4):
-            nc.scalar.dma_start(
-                out=ks_pool[32 * quad : 32 * quad + 4, :].bitcast(I32),
-                in_=k_scales[0, 4 * quad : 4 * quad + 4, :].bitcast(I32),
-            )
-        nc.scalar.activation(out=warm[:], in_=warm_in[:], func=ACT.Sigmoid)
+
+        nc.vector.memset(ks_pool[64:P, :].bitcast(I32), 0)
+        nc.vector.memset(ks_pool[32:64, :].bitcast(I32), 0)
+        nc.vector.memset(ks_plane[:].rearrange("f o n -> f (o n)").bitcast(I32), 0)
+        make_identity(nc, ident[:])
+        nc.gpsimd.memset(qsc[:].bitcast(I32), 0)
+        nc.gpsimd.memset(vsc_pool[:].bitcast(I32), 0)
         q_rows = q_scales.rearrange("b o f q -> f (b o) q").bitcast(I32)
         v_rows = v_scales.rearrange("u f e -> f u e").bitcast(I32)
         for quad in range(4):
@@ -81,29 +81,39 @@ def tile_attend_pkv4q_sigm_kernel(
                 out=qsc[32 * quad : 32 * quad + 4, :].bitcast(I32).rearrange("f (c q) -> f c q", c=B * PASSES),
                 in_=q_rows[4 * quad : 4 * quad + 4],
             )
-        make_identity(nc, ident[:])
         for quad in range(4):
-            nc.scalar.dma_start(
+            nc.gpsimd.dma_start(
                 out=vsc_pool[32 * quad : 32 * quad + 4, :].bitcast(I32).rearrange("f (u e) -> f u e", u=POOL_PAGES),
                 in_=v_rows[4 * quad : 4 * quad + 4],
             )
 
-        nc.vector.tensor_copy(vw_got[:], vw_pool[:].bitcast(U32).indirect(voffs_sb[:]))
         nc.vector.tensor_copy(ks_got[:], ks_pool[:].indirect(offs_sb[:]))
-        for quad in range(4):
-            nc.sync.dma_start(
-                out=ks_pass1[32 * quad : 32 * quad + 4, :].bitcast(I32),
-                in_=ks_got[32 * quad + 4 : 32 * quad + 32 : 8, :].bitcast(I32),
+        for o in range(PASSES):
+            for quad in range(4):
+                row = 16 * o + 4 * quad
+                nc.sync.dma_start(
+                    out=ks_plane[32 * quad : 32 * quad + 4, o, :].bitcast(I32),
+                    in_=ks_got[row : row + 4, :].bitcast(I32),
+                )
+
+        for m0 in range(0, FOLD, PACK):
+            spread = psum.tile([P, PACK, P], F32, name=f"spread{m0}", tag=f"turn{m0 // PACK % PAGES}")
+            for m in range(PACK):
+                nc.tensor.transpose(spread[:, m, :], vs_fold[:, m0 + m : m0 + m + 1].to_broadcast([P, P]), ident[:])
+            nc.scalar.copy(
+                out=vs_pool[:].rearrange("p (n m) -> p n m", m=FOLD)[:, :, m0 : m0 + PACK],
+                in_=spread[:].rearrange("p m n -> p n m"),
             )
-        vs_pool = reuse.tile([P, T], F32, name="vs_pool", align_bytes=64, offset=POOL_AT)
-        nc.sync.dma_start(out=vs_pool[:], in_=vs)
-        ks_plane = [ks_got, ks_pass1]
 
         kw_got = [
             reuse.tile([P, PAGE], U32, name=f"kw_got{e}", align_bytes=64, offset=(e % 2) * SLOT_BYTES)
             for e in range(PAGES)
         ]
-        vsc_got = reuse.tile([P, PAGES * DV], U8, name="vsc_got", align_bytes=64, offset=POOL_AT)
+        vw_got = reuse.tile([P, PAGES * DV], U32, name="vw_got", align_bytes=64, offset=POOL_AT)
+        vsc_got = [
+            reuse.tile([P, N // PAGE * DV], U8, name=f"vsc_got{b}", align_bytes=64, offset=POOL_AT + (b + 1) * SLOT_BYTES)
+            for b in range(B)
+        ]
         w_f32 = [
             reuse.tile([P, PAGE], F32, name=f"w_f32{e}", align_bytes=64, offset=e * SLOT_BYTES)
             if e < 2
@@ -114,11 +124,14 @@ def tile_attend_pkv4q_sigm_kernel(
         kw_part = [keep.tile([P, PASSES, PAGE], U16, name=f"kw_part{e}", align_bytes=64) for e in range(PAGES)]
         p_sb = [keep.tile([P, PAGE], F32, name=f"p_sb{e}", align_bytes=64) for e in range(PAGES)]
         w_bf = [keep.tile([P, NQ, PACK], BF16, name=f"w_bf{e}", align_bytes=64) for e in range(PAGES)]
-        w_codes = [keep.tile([P, NQ], U32, name=f"w_codes{e}", align_bytes=64) for e in range(PAGES)]
+        w_codes = [
+            reuse.tile([P, NQ], U32, name=f"w_codes{e}", align_bytes=64, offset=POOL_AT + 3 * SLOT_BYTES + 4 * NQ * e)
+            for e in range(PAGES)
+        ]
         w_scale = [keep.tile([P, NQ], U8, name=f"w_scale{e}", align_bytes=64) for e in range(PAGES)]
         score = [psum.tile([P, PAGE], F32, name=f"score{e}", tag=f"score{e % 2}") for e in range(2)]
-        w_turn = [psum.tile([P, 2, P], F32, name=f"w_turn{e}") for e in range(PAGES)]
-        y_ps = [psum.tile([P, DV], F32, name=f"y_ps{b}") for b in range(B)]
+        w_turn = [psum.tile([P, 2, P], F32, name=f"w_turn{e}", tag=f"turn{e}") for e in range(PAGES)]
+        y_ps = [psum.tile([P, DV], F32, name=f"y_ps{b}", tag=f"turn{PAGES - 1}" if b == 0 else "y_last") for b in range(B)]
 
         def gather_keys(e):
             cols = slice(e * PAGE // 16, (e + 1) * PAGE // 16)
@@ -136,7 +149,7 @@ def tile_attend_pkv4q_sigm_kernel(
                     lhsT=qw[:, q_cols].bitcast(FP8X4),
                     lhsT_scale=qsc[:, q_cols],
                     rhs=kw_part[e][:, o, :].bitcast(FP4X4),
-                    rhs_scale=ks_plane[o][:, e * PAGE : (e + 1) * PAGE],
+                    rhs_scale=ks_plane[:, o, e * PAGE : (e + 1) * PAGE],
                     start=(o == 0),
                     stop=(o == PASSES - 1),
                 )
@@ -169,7 +182,7 @@ def tile_attend_pkv4q_sigm_kernel(
                 lhsT=w_codes[e][:].bitcast(FP8X4),
                 lhsT_scale=w_scale[e][:],
                 rhs=vw_got[:, v_cols].bitcast(FP8X4),
-                rhs_scale=vsc_got[:, v_cols],
+                rhs_scale=vsc_got[b][:, first * DV : (first + 1) * DV],
                 start=(first == 0),
                 stop=(first == N // PAGE - 1),
             )
@@ -189,9 +202,11 @@ def tile_attend_pkv4q_sigm_kernel(
         for e in range(PAGES):
             weigh(e)
             turn(e)
-        nc.vector.tensor_copy(vsc_got[:], vsc_pool[:].indirect(voffs_sb[:]))
-        for e in range(PAGES):
-            quantise(e)
-            mix(e)
-            if e % 2 == 1:
-                store(e // 2)
+        nc.vector.tensor_copy(vw_got[:], vw_pool[:].bitcast(U32).indirect(voffs_sb[:]))
+        for b in range(B):
+            quantise(2 * b)
+            nc.vector.tensor_copy(vsc_got[b][:], vsc_pool[:].indirect(voffs_sb[:, 16 * b : 16 * (b + 1)]))
+            quantise(2 * b + 1)
+            mix(2 * b)
+            mix(2 * b + 1)
+            store(b)

@@ -11,7 +11,7 @@ PAGES = B * N // PAGE
 POOL_PAGES = T // PAGE
 PASSES = D // 512
 SLOT_BYTES = 4 * PAGE
-POOL_AT = 2 * SLOT_BYTES
+POOL_AT = 4 * SLOT_BYTES
 FOLD = T // P
 FLOPS = 2 * B * NQ * N * (D + DV)
 
@@ -39,9 +39,8 @@ def tile_attend_pkv4q_sigm_kernel(
         offs_sb = keep.tile([P, B * N // 16], U16, name="offs_sb")
         voffs_sb = keep.tile([P, PAGES * DV // 16], U16, name="voffs_sb")
         kw_pool = keep.tile([P, T], I32, name="kw_pool", align_bytes=64)
-        ks_pool = reuse.tile([P, T], U8, name="ks_pool", align_bytes=64, offset=0)
+        ks_pool = reuse.tile([P, T], U8, name="ks_pool", align_bytes=64, offset=SLOT_BYTES // 2)
         vs_pool = reuse.tile([P, T], F32, name="vs_pool", align_bytes=64, offset=POOL_AT)
-        vw_pool = keep.tile([P, POOL_PAGES * DV], I32, name="vw_pool", align_bytes=64)
         vsc_pool = keep.tile([P, POOL_PAGES * DV], U8, name="vsc_pool", align_bytes=64)
         qw = keep.tile([P, B * PASSES * NQ], I32, name="qw", align_bytes=64)
         qsc = keep.tile([P, B * PASSES * NQ], U8, name="qsc", align_bytes=64)
@@ -57,16 +56,12 @@ def tile_attend_pkv4q_sigm_kernel(
         nc.sync.dma_start(out=ks_pool[0:32, :].bitcast(I32), in_=k_scales.rearrange("o f t -> (o f) t").bitcast(I32))
         nc.sync.dma_start(offs_sb[:], offs)
         nc.sync.dma_start(out=vs_fold[:], in_=vs[0].rearrange("(n m) -> n m", m=FOLD))
-        nc.sync.dma_start(out=kw_pool[:], in_=k_words[0].rearrange("g t r -> g (t r)").bitcast(I32))
+        nc.sync.dma_start(voffs_sb[:], voffs)
         nc.sync.dma_start(
             out=qw[:].rearrange("g (c q) -> g c q", q=NQ),
             in_=q_words.rearrange("b o g q r -> g (b o) (q r)").bitcast(I32),
         )
-        nc.sync.dma_start(voffs_sb[:], voffs)
-        nc.sync.dma_start(
-            out=vw_pool[:].rearrange("g (u e) -> g u e", e=DV),
-            in_=v_words.rearrange("u g e r -> g u (e r)").bitcast(I32),
-        )
+        nc.sync.dma_start(out=kw_pool[:], in_=k_words[0].rearrange("g t r -> g (t r)").bitcast(I32))
 
         nc.vector.memset(ks_pool[64:P, :].bitcast(I32), 0)
         nc.vector.memset(ks_pool[32:64, :].bitcast(I32), 0)
@@ -95,6 +90,11 @@ def tile_attend_pkv4q_sigm_kernel(
                     out=ks_plane[32 * quad : 32 * quad + 4, o, :].bitcast(I32),
                     in_=ks_got[row : row + 4, :].bitcast(I32),
                 )
+        vw_pool = reuse.tile([P, POOL_PAGES * DV], I32, name="vw_pool", align_bytes=64, offset=2 * SLOT_BYTES)
+        nc.sync.dma_start(
+            out=vw_pool[:].rearrange("g (u e) -> g u e", e=DV),
+            in_=v_words.rearrange("u g e r -> g u (e r)").bitcast(I32),
+        )
 
         for m0 in range(0, FOLD, PACK):
             spread = psum.tile([P, PACK, P], F32, name=f"spread{m0}", tag=f"turn{m0 // PACK % PAGES}")
@@ -156,11 +156,17 @@ def tile_attend_pkv4q_sigm_kernel(
             nc.scalar.activation(out=p_sb[e][:], in_=score[e % 2][:], func=ACT.Sigmoid)
 
         def weigh(e):
-            cols = slice(e * PAGE // 16, (e + 1) * PAGE // 16)
-            nc.vector.tensor_tensor(w_f32[e][:], vs_pool[:].indirect(offs_sb[:, cols]), p_sb[e][:], MULT)
+            step = PAGE // 2 if e == PAGES - 1 else PAGE
+            for s0 in range(0, PAGE, step):
+                cols = slice((e * PAGE + s0) // 16, (e * PAGE + s0 + step) // 16)
+                slots = slice(s0, s0 + step)
+                nc.vector.tensor_tensor(w_f32[e][:, slots], vs_pool[:].indirect(offs_sb[:, cols]), p_sb[e][:, slots], MULT)
+                nc.scalar.copy(
+                    out=w_pair[e][:, :, s0 // PACK : (s0 + step) // PACK, :],
+                    in_=w_f32[e][:, slots].rearrange("q (m u r) -> q u m r", u=2, r=2),
+                )
 
         def turn(e):
-            nc.scalar.copy(out=w_pair[e][:], in_=w_f32[e][:].rearrange("q (m u r) -> q u m r", u=2, r=2))
             words = w_pair[e][:].rearrange("q u m r -> q (u m r)").bitcast(F32)
             for u in range(2):
                 nc.tensor.transpose(w_turn[e][:, u, :], words[:, u * P : (u + 1) * P], ident[:])

@@ -11,7 +11,10 @@ PAGES = B * N // PAGE
 POOL_PAGES = T // PAGE
 PASSES = D // 512
 SLOT_BYTES = 4 * PAGE
-POOL_AT = 4 * SLOT_BYTES
+KS_AT = SLOT_BYTES - 512
+VSC_AT = 2 * SLOT_BYTES
+VW_AT = VSC_AT + POOL_PAGES * DV
+POOL_AT = VW_AT + 4 * POOL_PAGES * DV
 FOLD = T // P
 FLOPS = 2 * B * NQ * N * (D + DV)
 
@@ -39,13 +42,13 @@ def tile_attend_pkv4q_sigm_kernel(
         offs_sb = keep.tile([P, B * N // 16], U16, name="offs_sb")
         voffs_sb = keep.tile([P, PAGES * DV // 16], U16, name="voffs_sb")
         kw_pool = keep.tile([P, T], I32, name="kw_pool", align_bytes=64)
-        ks_pool = reuse.tile([P, T], U8, name="ks_pool", align_bytes=64, offset=SLOT_BYTES // 2)
+        ks_pool = reuse.tile([P, T], U8, name="ks_pool", align_bytes=64, offset=KS_AT)
         vs_pool = reuse.tile([P, T], F32, name="vs_pool", align_bytes=64, offset=POOL_AT)
-        vsc_pool = keep.tile([P, POOL_PAGES * DV], U8, name="vsc_pool", align_bytes=64)
         qw = keep.tile([P, B * PASSES * NQ], I32, name="qw", align_bytes=64)
         qsc = keep.tile([P, B * PASSES * NQ], U8, name="qsc", align_bytes=64)
         ks_got = keep.tile([P, B * N], U8, name="ks_got", align_bytes=64)
         ks_plane = keep.tile([P, PASSES, B * N], U8, name="ks_plane", align_bytes=64)
+        vs_rows = keep.tile([P, P], F32, name="vs_rows")
         vs_fold = keep.tile([P, FOLD], F32, name="vs_fold")
         ident = keep.tile([P, P], F32, name="ident")
         warm_in = keep.tile([P, 8], F32, name="warm_in")
@@ -55,7 +58,7 @@ def tile_attend_pkv4q_sigm_kernel(
 
         nc.sync.dma_start(out=ks_pool[0:32, :].bitcast(I32), in_=k_scales.rearrange("o f t -> (o f) t").bitcast(I32))
         nc.sync.dma_start(offs_sb[:], offs)
-        nc.sync.dma_start(out=vs_fold[:], in_=vs[0].rearrange("(n m) -> n m", m=FOLD))
+        nc.sync.dma_start(out=vs_rows[:], in_=vs[0 : P // FOLD].rearrange("a (m n) -> (a m) n", n=P))
         nc.sync.dma_start(voffs_sb[:], voffs)
         nc.sync.dma_start(
             out=qw[:].rearrange("g (c q) -> g c q", q=NQ),
@@ -65,21 +68,15 @@ def tile_attend_pkv4q_sigm_kernel(
 
         nc.vector.memset(ks_pool[64:P, :].bitcast(I32), 0)
         nc.vector.memset(ks_pool[32:64, :].bitcast(I32), 0)
-        nc.vector.memset(ks_plane[:].rearrange("f o n -> f (o n)").bitcast(I32), 0)
-        make_identity(nc, ident[:])
         nc.gpsimd.memset(qsc[:].bitcast(I32), 0)
-        nc.gpsimd.memset(vsc_pool[:].bitcast(I32), 0)
+        make_identity(nc, ident[:])
+        nc.gpsimd.memset(ks_plane[:].rearrange("f o n -> f (o n)").bitcast(I32), 0)
         q_rows = q_scales.rearrange("b o f q -> f (b o) q").bitcast(I32)
         v_rows = v_scales.rearrange("u f e -> f u e").bitcast(I32)
         for quad in range(4):
             nc.gpsimd.dma_start(
                 out=qsc[32 * quad : 32 * quad + 4, :].bitcast(I32).rearrange("f (c q) -> f c q", c=B * PASSES),
                 in_=q_rows[4 * quad : 4 * quad + 4],
-            )
-        for quad in range(4):
-            nc.gpsimd.dma_start(
-                out=vsc_pool[32 * quad : 32 * quad + 4, :].bitcast(I32).rearrange("f (u e) -> f u e", u=POOL_PAGES),
-                in_=v_rows[4 * quad : 4 * quad + 4],
             )
 
         nc.vector.tensor_copy(ks_got[:], ks_pool[:].indirect(offs_sb[:]))
@@ -90,30 +87,34 @@ def tile_attend_pkv4q_sigm_kernel(
                     out=ks_plane[32 * quad : 32 * quad + 4, o, :].bitcast(I32),
                     in_=ks_got[row : row + 4, :].bitcast(I32),
                 )
-        vw_pool = reuse.tile([P, POOL_PAGES * DV], I32, name="vw_pool", align_bytes=64, offset=2 * SLOT_BYTES)
+        vw_pool = reuse.tile([P, POOL_PAGES * DV], I32, name="vw_pool", align_bytes=64, offset=VW_AT)
         nc.sync.dma_start(
             out=vw_pool[:].rearrange("g (u e) -> g u e", e=DV),
             in_=v_words.rearrange("u g e r -> g u (e r)").bitcast(I32),
         )
+        vsc_pool = reuse.tile([P, POOL_PAGES * DV], U8, name="vsc_pool", align_bytes=64, offset=VSC_AT)
+        nc.gpsimd.memset(vsc_pool[:].bitcast(I32), 0)
+        for quad in range(4):
+            nc.sync.dma_start(
+                out=vsc_pool[32 * quad : 32 * quad + 4, :].bitcast(I32).rearrange("f (u e) -> f u e", u=POOL_PAGES),
+                in_=v_rows[4 * quad : 4 * quad + 4],
+            )
 
+        fold_ps = psum.tile([P, P], F32, name="fold_ps", tag="y_last")
+        nc.tensor.transpose(fold_ps[:], vs_rows[:], ident[:])
+        nc.scalar.copy(out=vs_fold[:], in_=fold_ps[:, 0:FOLD])
         for m0 in range(0, FOLD, PACK):
             spread = psum.tile([P, PACK, P], F32, name=f"spread{m0}", tag=f"turn{m0 // PACK % PAGES}")
             for m in range(PACK):
                 nc.tensor.transpose(spread[:, m, :], vs_fold[:, m0 + m : m0 + m + 1].to_broadcast([P, P]), ident[:])
-            nc.scalar.copy(
-                out=vs_pool[:].rearrange("p (n m) -> p n m", m=FOLD)[:, :, m0 : m0 + PACK],
-                in_=spread[:].rearrange("p m n -> p n m"),
-            )
+            nc.scalar.copy(out=vs_pool[:, m0 * P : (m0 + PACK) * P], in_=spread[:].rearrange("p m n -> p (m n)"))
 
         kw_got = [
             reuse.tile([P, PAGE], U32, name=f"kw_got{e}", align_bytes=64, offset=(e % 2) * SLOT_BYTES)
             for e in range(PAGES)
         ]
         vw_got = reuse.tile([P, PAGES * DV], U32, name="vw_got", align_bytes=64, offset=POOL_AT)
-        vsc_got = [
-            reuse.tile([P, N // PAGE * DV], U8, name=f"vsc_got{b}", align_bytes=64, offset=POOL_AT + (b + 1) * SLOT_BYTES)
-            for b in range(B)
-        ]
+        vsc_got = reuse.tile([P, PAGES * DV], U8, name="vsc_got", align_bytes=64, offset=POOL_AT + SLOT_BYTES)
         w_f32 = [
             reuse.tile([P, PAGE], F32, name=f"w_f32{e}", align_bytes=64, offset=e * SLOT_BYTES)
             if e < 2
@@ -123,12 +124,9 @@ def tile_attend_pkv4q_sigm_kernel(
         w_pair = [keep.tile([P, 2, P, 2], BF16, name=f"w_pair{e}", align_bytes=64) for e in range(PAGES)]
         kw_part = [keep.tile([P, PASSES, PAGE], U16, name=f"kw_part{e}", align_bytes=64) for e in range(PAGES)]
         p_sb = [keep.tile([P, PAGE], F32, name=f"p_sb{e}", align_bytes=64) for e in range(PAGES)]
-        w_bf = [keep.tile([P, NQ, PACK], BF16, name=f"w_bf{e}", align_bytes=64) for e in range(PAGES)]
-        w_codes = [
-            reuse.tile([P, NQ], U32, name=f"w_codes{e}", align_bytes=64, offset=POOL_AT + 3 * SLOT_BYTES + 4 * NQ * e)
-            for e in range(PAGES)
-        ]
-        w_scale = [keep.tile([P, NQ], U8, name=f"w_scale{e}", align_bytes=64) for e in range(PAGES)]
+        w_bf = keep.tile([P, PAGES, NQ * PACK], BF16, name="w_bf", align_bytes=64)
+        w_codes = reuse.tile([P, PAGES * NQ], U32, name="w_codes", align_bytes=64, offset=POOL_AT + 2 * SLOT_BYTES)
+        w_scale = keep.tile([P, PAGES * NQ], U8, name="w_scale", align_bytes=64)
         score = [psum.tile([P, PAGE], F32, name=f"score{e}", tag=f"score{e % 2}") for e in range(2)]
         w_turn = [psum.tile([P, 2, P], F32, name=f"w_turn{e}", tag=f"turn{e}") for e in range(PAGES)]
         y_ps = [psum.tile([P, DV], F32, name=f"y_ps{b}", tag=f"turn{PAGES - 1}" if b == 0 else "y_last") for b in range(B)]
@@ -171,13 +169,16 @@ def tile_attend_pkv4q_sigm_kernel(
             for u in range(2):
                 nc.tensor.transpose(w_turn[e][:, u, :], words[:, u * P : (u + 1) * P], ident[:])
             nc.scalar.copy(
-                out=w_bf[e][:].rearrange("m q t -> m (q t)").bitcast(F32).rearrange("m (q u) -> m q u", u=2),
+                out=w_bf[:, e, :].bitcast(F32).rearrange("m (q u) -> m q u", u=2),
                 in_=w_turn[e][:].rearrange("m u q -> m q u"),
             )
 
-        def quantise(e):
+        def quantise(first, last):
+            cols = slice(first * NQ, (last + 1) * NQ)
             nc.vector.quantize_mx(
-                out=w_codes[e][:].bitcast(FP8X4), scales=w_scale[e][:], in_=w_bf[e][:].rearrange("m q t -> m (q t)")
+                out=w_codes[:, cols].bitcast(FP8X4),
+                scales=w_scale[:, cols],
+                in_=w_bf[:, first : last + 1, :].rearrange("m e c -> m (e c)"),
             )
 
         def mix(e):
@@ -185,10 +186,10 @@ def tile_attend_pkv4q_sigm_kernel(
             v_cols = slice(e * DV, (e + 1) * DV)
             nc.tensor.matmul_mx(
                 out=y_ps[b][:],
-                lhsT=w_codes[e][:].bitcast(FP8X4),
-                lhsT_scale=w_scale[e][:],
+                lhsT=w_codes[:, e * NQ : (e + 1) * NQ].bitcast(FP8X4),
+                lhsT_scale=w_scale[:, e * NQ : (e + 1) * NQ],
                 rhs=vw_got[:, v_cols].bitcast(FP8X4),
-                rhs_scale=vsc_got[b][:, first * DV : (first + 1) * DV],
+                rhs_scale=vsc_got[:, v_cols],
                 start=(first == 0),
                 stop=(first == N // PAGE - 1),
             )
@@ -209,10 +210,13 @@ def tile_attend_pkv4q_sigm_kernel(
             weigh(e)
             turn(e)
         nc.vector.tensor_copy(vw_got[:], vw_pool[:].bitcast(U32).indirect(voffs_sb[:]))
-        for b in range(B):
-            quantise(2 * b)
-            nc.vector.tensor_copy(vsc_got[b][:], vsc_pool[:].indirect(voffs_sb[:, 16 * b : 16 * (b + 1)]))
-            quantise(2 * b + 1)
-            mix(2 * b)
-            mix(2 * b + 1)
-            store(b)
+        nc.vector.tensor_copy(vsc_got[:], vsc_pool[:].indirect(voffs_sb[:]))
+        quantise(2, 2)
+        mix(2)
+        quantise(0, 1)
+        mix(0)
+        mix(1)
+        store(0)
+        quantise(3, 3)
+        mix(3)
+        store(1)

@@ -16,6 +16,7 @@ VSC_AT = 2 * SLOT_BYTES
 VW_AT = VSC_AT + POOL_PAGES * DV
 POOL_AT = VW_AT + 4 * POOL_PAGES * DV
 FOLD = T // P
+KS_ROW = 96
 FLOPS = 2 * B * NQ * N * (D + DV)
 
 F32 = mybir.dt.float32
@@ -48,41 +49,36 @@ def tile_attend_pkv4q_sigm_kernel(
         qsc = keep.tile([P, B * PASSES * NQ], U8, name="qsc", align_bytes=64)
         ks_got = keep.tile([P, B * N], U8, name="ks_got", align_bytes=64)
         ks_plane = keep.tile([P, PASSES, B * N], U8, name="ks_plane", align_bytes=64)
-        vs_rows = keep.tile([P, P], F32, name="vs_rows")
         vs_fold = keep.tile([P, FOLD], F32, name="vs_fold")
         ident = keep.tile([P, P], F32, name="ident")
-        warm_in = keep.tile([P, 8], F32, name="warm_in")
-        warm = keep.tile([P, 8], F32, name="warm")
-        nc.gpsimd.memset(warm_in[:], 0.0)
-        nc.scalar.activation(out=warm[:], in_=warm_in[:], func=ACT.Sigmoid)
 
-        nc.sync.dma_start(out=ks_pool[0:32, :].bitcast(I32), in_=k_scales.rearrange("o f t -> (o f) t").bitcast(I32))
+        nc.gpsimd.memset(qsc[:].bitcast(I32), 0)
+        nc.sync.dma_start(out=ks_pool[KS_ROW:P, :].bitcast(I32), in_=k_scales.rearrange("o f t -> (o f) t").bitcast(I32))
         nc.sync.dma_start(offs_sb[:], offs)
-        nc.sync.dma_start(out=vs_rows[:], in_=vs[0 : P // FOLD].rearrange("a (m n) -> (a m) n", n=P))
-        nc.sync.dma_start(voffs_sb[:], voffs)
-        nc.sync.dma_start(
-            out=qw[:].rearrange("g (c q) -> g c q", q=NQ),
-            in_=q_words.rearrange("b o g q r -> g (b o) (q r)").bitcast(I32),
-        )
+        nc.sync.dma_start(out=vs_fold[:], in_=vs[0:1].rearrange("a (n m) -> (a n) m", m=FOLD))
         nc.sync.dma_start(out=kw_pool[:], in_=k_words[0].rearrange("g t r -> g (t r)").bitcast(I32))
 
-        nc.vector.memset(ks_pool[64:P, :].bitcast(I32), 0)
-        nc.vector.memset(ks_pool[32:64, :].bitcast(I32), 0)
-        nc.gpsimd.memset(qsc[:].bitcast(I32), 0)
+        nc.vector.memset(ks_pool[0:KS_ROW, :].bitcast(I32), 0)
         make_identity(nc, ident[:])
         nc.gpsimd.memset(ks_plane[:].rearrange("f o n -> f (o n)").bitcast(I32), 0)
         q_rows = q_scales.rearrange("b o f q -> f (b o) q").bitcast(I32)
         v_rows = v_scales.rearrange("u f e -> f u e").bitcast(I32)
         for quad in range(4):
-            nc.gpsimd.dma_start(
+            nc.sync.dma_start(
                 out=qsc[32 * quad : 32 * quad + 4, :].bitcast(I32).rearrange("f (c q) -> f c q", c=B * PASSES),
                 in_=q_rows[4 * quad : 4 * quad + 4],
             )
 
+
+        nc.sync.dma_start(
+            out=qw[:].rearrange("g (c q) -> g c q", q=NQ),
+            in_=q_words.rearrange("b o g q r -> g (b o) (q r)").bitcast(I32),
+        )
+        nc.sync.dma_start(voffs_sb[:], voffs)
         nc.vector.tensor_copy(ks_got[:], ks_pool[:].indirect(offs_sb[:]))
         for o in range(PASSES):
             for quad in range(4):
-                row = 16 * o + 4 * quad
+                row = KS_ROW + 16 * o + 4 * quad
                 nc.sync.dma_start(
                     out=ks_plane[32 * quad : 32 * quad + 4, o, :].bitcast(I32),
                     in_=ks_got[row : row + 4, :].bitcast(I32),
@@ -100,14 +96,14 @@ def tile_attend_pkv4q_sigm_kernel(
                 in_=v_rows[4 * quad : 4 * quad + 4],
             )
 
-        fold_ps = psum.tile([P, P], F32, name="fold_ps", tag="y_last")
-        nc.tensor.transpose(fold_ps[:], vs_rows[:], ident[:])
-        nc.scalar.copy(out=vs_fold[:], in_=fold_ps[:, 0:FOLD])
         for m0 in range(0, FOLD, PACK):
             spread = psum.tile([P, PACK, P], F32, name=f"spread{m0}", tag=f"turn{m0 // PACK % PAGES}")
             for m in range(PACK):
                 nc.tensor.transpose(spread[:, m, :], vs_fold[:, m0 + m : m0 + m + 1].to_broadcast([P, P]), ident[:])
-            nc.scalar.copy(out=vs_pool[:, m0 * P : (m0 + PACK) * P], in_=spread[:].rearrange("p m n -> p (m n)"))
+            nc.scalar.copy(
+                out=vs_pool[:].rearrange("p (n m) -> p n m", m=FOLD)[:, :, m0 : m0 + PACK],
+                in_=spread[:].rearrange("p m n -> p n m"),
+            )
 
         kw_got = [
             reuse.tile([P, PAGE], U32, name=f"kw_got{e}", align_bytes=64, offset=(e % 2) * SLOT_BYTES)

@@ -15,6 +15,7 @@ KS_AT = SLOT_BYTES - 512
 VSC_AT = 2 * SLOT_BYTES
 VW_AT = VSC_AT + POOL_PAGES * DV
 POOL_AT = VW_AT + 4 * POOL_PAGES * DV
+LAST_AT = POOL_AT + 4 * T
 FOLD = T // P
 KS_ROW = 96
 FLOPS = 2 * B * NQ * N * (D + DV)
@@ -96,14 +97,14 @@ def tile_attend_pkv4q_sigm_kernel(
                 in_=v_rows[4 * quad : 4 * quad + 4],
             )
 
-        for m0 in range(0, FOLD, PACK):
-            spread = psum.tile([P, PACK, P], F32, name=f"spread{m0}", tag=f"turn{m0 // PACK % PAGES}")
-            for m in range(PACK):
-                nc.tensor.transpose(spread[:, m, :], vs_fold[:, m0 + m : m0 + m + 1].to_broadcast([P, P]), ident[:])
-            nc.scalar.copy(
-                out=vs_pool[:].rearrange("p (n m) -> p n m", m=FOLD)[:, :, m0 : m0 + PACK],
-                in_=spread[:].rearrange("p m n -> p n m"),
-            )
+        dealt = vs_pool[:].rearrange("p (u r n h j) -> p r h u n j", u=POOL_PAGES, r=PACK, h=2, j=PACK)
+        for r in range(PACK):
+            for h in range(2):
+                spread = psum.tile([P, PACK, P], F32, name=f"spread{r}_{h}", tag=f"turn{(2 * r + h) % PAGES}")
+                for j in range(PACK):
+                    m = PACK * (PACK * h + j) + r
+                    nc.tensor.transpose(spread[:, j, :], vs_fold[:, m : m + 1].to_broadcast([P, P]), ident[:])
+                nc.scalar.copy(out=dealt[:, r, h], in_=spread[:].rearrange("p j (u n) -> p u n j", u=POOL_PAGES))
 
         kw_got = [
             reuse.tile([P, PAGE], U32, name=f"kw_got{e}", align_bytes=64, offset=(e % 2) * SLOT_BYTES)
@@ -114,18 +115,19 @@ def tile_attend_pkv4q_sigm_kernel(
         w_f32 = [
             reuse.tile([P, PAGE], F32, name=f"w_f32{e}", align_bytes=64, offset=e * SLOT_BYTES)
             if e < 2
+            else reuse.tile([P, PAGE], F32, name=f"w_f32{e}", align_bytes=64, offset=LAST_AT)
+            if e == PAGES - 1
             else keep.tile([P, PAGE], F32, name=f"w_f32{e}", align_bytes=64)
             for e in range(PAGES)
         ]
-        w_pair = [keep.tile([P, 2, P, 2], BF16, name=f"w_pair{e}", align_bytes=64) for e in range(PAGES)]
         kw_part = [keep.tile([P, PASSES, PAGE], U16, name=f"kw_part{e}", align_bytes=64) for e in range(PAGES)]
         p_sb = [keep.tile([P, PAGE], F32, name=f"p_sb{e}", align_bytes=64) for e in range(PAGES)]
         w_bf = keep.tile([P, PAGES, NQ * PACK], BF16, name="w_bf", align_bytes=64)
-        w_codes = reuse.tile([P, PAGES * NQ], U32, name="w_codes", align_bytes=64, offset=POOL_AT + 2 * SLOT_BYTES)
+        w_codes = reuse.tile([P, PAGES * NQ], U32, name="w_codes", align_bytes=64, offset=LAST_AT)
         w_scale = keep.tile([P, PAGES * NQ], U8, name="w_scale", align_bytes=64)
-        score = [psum.tile([P, PAGE], F32, name=f"score{e}", tag=f"score{e % 2}") for e in range(2)]
-        w_turn = [psum.tile([P, 2, P], F32, name=f"w_turn{e}", tag=f"turn{e}") for e in range(PAGES)]
-        y_ps = [psum.tile([P, DV], F32, name=f"y_ps{b}", tag=f"turn{PAGES - 1}" if b == 0 else "y_last") for b in range(B)]
+        score = [psum.tile([P, PAGE], F32, name=f"score{e}", tag=f"score{e % 2}") for e in range(PAGES)]
+        w_turn = [psum.tile([P, PACK, P], F32, name=f"w_turn{e}", tag=f"turn{e}") for e in range(PAGES)]
+        y_ps = [psum.tile([P, DV], F32, name=f"y_ps{b}", tag=f"y{b}") for b in range(B)]
 
         def gather_keys(e):
             cols = slice(e * PAGE // 16, (e + 1) * PAGE // 16)
@@ -139,7 +141,7 @@ def tile_attend_pkv4q_sigm_kernel(
             for o in range(PASSES):
                 q_cols = slice((b * PASSES + o) * NQ, (b * PASSES + o + 1) * NQ)
                 nc.tensor.matmul_mx(
-                    out=score[e % 2][:],
+                    out=score[e][:],
                     lhsT=qw[:, q_cols].bitcast(FP8X4),
                     lhsT_scale=qsc[:, q_cols],
                     rhs=kw_part[e][:, o, :].bitcast(FP4X4),
@@ -147,7 +149,13 @@ def tile_attend_pkv4q_sigm_kernel(
                     start=(o == 0),
                     stop=(o == PASSES - 1),
                 )
-            nc.scalar.activation(out=p_sb[e][:], in_=score[e % 2][:], func=ACT.Sigmoid)
+            step = PACK // 2 if e == PAGES - 1 else PACK
+            for r0 in range(0, PACK, step):
+                nc.scalar.activation(
+                    out=p_sb[e][:].rearrange("q (r s) -> q r s", r=PACK)[:, r0 : r0 + step, :],
+                    in_=score[e][:].rearrange("q (s r) -> q r s", r=PACK)[:, r0 : r0 + step, :],
+                    func=ACT.Sigmoid,
+                )
 
         def weigh(e):
             step = PAGE // 2 if e == PAGES - 1 else PAGE
@@ -155,18 +163,13 @@ def tile_attend_pkv4q_sigm_kernel(
                 cols = slice((e * PAGE + s0) // 16, (e * PAGE + s0 + step) // 16)
                 slots = slice(s0, s0 + step)
                 nc.vector.tensor_tensor(w_f32[e][:, slots], vs_pool[:].indirect(offs_sb[:, cols]), p_sb[e][:, slots], MULT)
-                nc.scalar.copy(
-                    out=w_pair[e][:, :, s0 // PACK : (s0 + step) // PACK, :],
-                    in_=w_f32[e][:, slots].rearrange("q (m u r) -> q u m r", u=2, r=2),
-                )
 
         def turn(e):
-            words = w_pair[e][:].rearrange("q u m r -> q (u m r)").bitcast(F32)
-            for u in range(2):
-                nc.tensor.transpose(w_turn[e][:, u, :], words[:, u * P : (u + 1) * P], ident[:])
+            for r in range(PACK):
+                nc.tensor.transpose(w_turn[e][:, r, :], w_f32[e][:, r * P : (r + 1) * P], ident[:])
             nc.scalar.copy(
-                out=w_bf[:, e, :].bitcast(F32).rearrange("m (q u) -> m q u", u=2),
-                in_=w_turn[e][:].rearrange("m u q -> m q u"),
+                out=w_bf[:, e, :].rearrange("s (q r) -> s q r", r=PACK),
+                in_=w_turn[e][:].rearrange("s r q -> s q r"),
             )
 
         def quantise(first, last):
@@ -207,12 +210,12 @@ def tile_attend_pkv4q_sigm_kernel(
             turn(e)
         nc.vector.tensor_copy(vw_got[:], vw_pool[:].bitcast(U32).indirect(voffs_sb[:]))
         nc.vector.tensor_copy(vsc_got[:], vsc_pool[:].indirect(voffs_sb[:]))
-        quantise(2, 2)
-        mix(2)
         quantise(0, 1)
         mix(0)
         mix(1)
         store(0)
+        quantise(2, 2)
+        mix(2)
         quantise(3, 3)
         mix(3)
         store(1)

@@ -16,6 +16,7 @@ VSC_AT = 2 * SLOT_BYTES
 VW_AT = VSC_AT + POOL_PAGES * DV
 POOL_AT = VW_AT + 4 * POOL_PAGES * DV
 LAST_AT = POOL_AT + 4 * T
+HALF_AT = LAST_AT + SLOT_BYTES
 FOLD = T // P
 KS_ROW = 96
 FLOPS = 2 * B * NQ * N * (D + DV)
@@ -49,7 +50,7 @@ def tile_attend_pkv4q_sigm_kernel(
         qw = keep.tile([P, B * PASSES * NQ], I32, name="qw", align_bytes=64)
         qsc = keep.tile([P, B * PASSES * NQ], U8, name="qsc", align_bytes=64)
         ks_got = keep.tile([P, B * N], U8, name="ks_got", align_bytes=64)
-        ks_plane = keep.tile([P, PASSES, B * N], U8, name="ks_plane", align_bytes=64)
+        ks_plane = [keep.tile([P, B * N], U8, name=f"ks_plane{o}", align_bytes=64) for o in range(PASSES)]
         vs_fold = keep.tile([P, FOLD], F32, name="vs_fold")
         ident = keep.tile([P, P], F32, name="ident")
 
@@ -61,7 +62,8 @@ def tile_attend_pkv4q_sigm_kernel(
 
         nc.vector.memset(ks_pool[0:KS_ROW, :].bitcast(I32), 0)
         make_identity(nc, ident[:])
-        nc.gpsimd.memset(ks_plane[:].rearrange("f o n -> f (o n)").bitcast(I32), 0)
+        for o in range(PASSES):
+            nc.gpsimd.memset(ks_plane[o][:].bitcast(I32), 0)
         q_rows = q_scales.rearrange("b o f q -> f (b o) q").bitcast(I32)
         v_rows = v_scales.rearrange("u f e -> f u e").bitcast(I32)
         for quad in range(4):
@@ -81,7 +83,7 @@ def tile_attend_pkv4q_sigm_kernel(
             for quad in range(4):
                 row = KS_ROW + 16 * o + 4 * quad
                 nc.sync.dma_start(
-                    out=ks_plane[32 * quad : 32 * quad + 4, o, :].bitcast(I32),
+                    out=ks_plane[o][32 * quad : 32 * quad + 4, :].bitcast(I32),
                     in_=ks_got[row : row + 4, :].bitcast(I32),
                 )
         vw_pool = reuse.tile([P, POOL_PAGES * DV], I32, name="vw_pool", align_bytes=64, offset=VW_AT)
@@ -110,7 +112,7 @@ def tile_attend_pkv4q_sigm_kernel(
             reuse.tile([P, PAGE], U32, name=f"kw_got{e}", align_bytes=64, offset=(e % 2) * SLOT_BYTES)
             for e in range(PAGES)
         ]
-        vw_got = reuse.tile([P, PAGES * DV], U32, name="vw_got", align_bytes=64, offset=POOL_AT)
+        vw_got = reuse.tile([P, PAGES * DV], U32, name="vw_got", align_bytes=64, offset=HALF_AT)
         vsc_got = reuse.tile([P, PAGES * DV], U8, name="vsc_got", align_bytes=64, offset=POOL_AT + SLOT_BYTES)
         w_f32 = [
             reuse.tile([P, PAGE], F32, name=f"w_f32{e}", align_bytes=64, offset=e * SLOT_BYTES)
@@ -121,7 +123,13 @@ def tile_attend_pkv4q_sigm_kernel(
             for e in range(PAGES)
         ]
         kw_part = [keep.tile([P, PASSES, PAGE], U16, name=f"kw_part{e}", align_bytes=64) for e in range(PAGES)]
-        p_sb = [keep.tile([P, PAGE], F32, name=f"p_sb{e}", align_bytes=64) for e in range(PAGES)]
+        pieces = [(e, 0, PACK) for e in range(PAGES - 1)] + [(PAGES - 1, r0, PACK // 2) for r0 in (0, PACK // 2)]
+        p_sb = {
+            (e, r0): reuse.tile([P, count * P], F32, name=f"p_sb{e}_{r0}", align_bytes=64, offset=HALF_AT)
+            if (e, r0) == (PAGES - 1, 0)
+            else keep.tile([P, count * P], F32, name=f"p_sb{e}_{r0}", align_bytes=64)
+            for e, r0, count in pieces
+        }
         w_bf = keep.tile([P, PAGES, NQ * PACK], BF16, name="w_bf", align_bytes=64)
         w_codes = reuse.tile([P, PAGES * NQ], U32, name="w_codes", align_bytes=64, offset=LAST_AT)
         w_scale = keep.tile([P, PAGES * NQ], U8, name="w_scale", align_bytes=64)
@@ -145,14 +153,14 @@ def tile_attend_pkv4q_sigm_kernel(
                     lhsT=qw[:, q_cols].bitcast(FP8X4),
                     lhsT_scale=qsc[:, q_cols],
                     rhs=kw_part[e][:, o, :].bitcast(FP4X4),
-                    rhs_scale=ks_plane[:, o, e * PAGE : (e + 1) * PAGE],
+                    rhs_scale=ks_plane[o][:, e * PAGE : (e + 1) * PAGE],
                     start=(o == 0),
                     stop=(o == PASSES - 1),
                 )
             step = PACK // 2 if e == PAGES - 1 else PACK
             for r0 in range(0, PACK, step):
                 nc.scalar.activation(
-                    out=p_sb[e][:].rearrange("q (r s) -> q r s", r=PACK)[:, r0 : r0 + step, :],
+                    out=p_sb[e, r0][:].rearrange("q (r s) -> q r s", r=step),
                     in_=score[e][:].rearrange("q (s r) -> q r s", r=PACK)[:, r0 : r0 + step, :],
                     func=ACT.Sigmoid,
                 )
@@ -162,7 +170,7 @@ def tile_attend_pkv4q_sigm_kernel(
             for s0 in range(0, PAGE, step):
                 cols = slice((e * PAGE + s0) // 16, (e * PAGE + s0 + step) // 16)
                 slots = slice(s0, s0 + step)
-                nc.vector.tensor_tensor(w_f32[e][:, slots], vs_pool[:].indirect(offs_sb[:, cols]), p_sb[e][:, slots], MULT)
+                nc.vector.tensor_tensor(w_f32[e][:, slots], vs_pool[:].indirect(offs_sb[:, cols]), p_sb[e, s0 // P][:], MULT)
 
         def turn(e):
             for r in range(PACK):

@@ -13,7 +13,8 @@ PASSES = D // 512
 SLOT_BYTES = 4 * PAGE
 KS_AT = SLOT_BYTES - 512
 VSC_AT = 2 * SLOT_BYTES
-VW_AT = VSC_AT + POOL_PAGES * DV
+QW_LATE_AT = VSC_AT + POOL_PAGES * DV
+VW_AT = QW_LATE_AT + 4 * PASSES * NQ
 POOL_AT = VW_AT + 4 * POOL_PAGES * DV
 LAST_AT = POOL_AT + 4 * T
 HALF_AT = LAST_AT + SLOT_BYTES
@@ -47,9 +48,9 @@ def tile_attend_pkv4q_sigm_kernel(
         kw_pool = keep.tile([P, T], I32, name="kw_pool", align_bytes=64)
         ks_pool = reuse.tile([P, T], U8, name="ks_pool", align_bytes=64, offset=KS_AT)
         vs_pool = reuse.tile([P, T], F32, name="vs_pool", align_bytes=64, offset=POOL_AT)
-        qw = keep.tile([P, B * PASSES * NQ], I32, name="qw", align_bytes=64)
+        qw_first = keep.tile([P, PASSES * NQ], I32, name="qw_first", align_bytes=64)
         qsc = keep.tile([P, B * PASSES * NQ], U8, name="qsc", align_bytes=64)
-        ks_got = keep.tile([P, B * N], U8, name="ks_got", align_bytes=64)
+        ks_got = reuse.tile([P, B * N], U8, name="ks_got", align_bytes=64, offset=VW_AT)
         ks_plane = [keep.tile([P, B * N], U8, name=f"ks_plane{o}", align_bytes=64) for o in range(PASSES)]
         vs_fold = keep.tile([P, FOLD], F32, name="vs_fold")
         ident = keep.tile([P, P], F32, name="ident")
@@ -59,6 +60,7 @@ def tile_attend_pkv4q_sigm_kernel(
         nc.sync.dma_start(offs_sb[:], offs)
         nc.sync.dma_start(out=vs_fold[:], in_=vs[0:1].rearrange("a (n m) -> (a n) m", m=FOLD))
         nc.sync.dma_start(out=kw_pool[:], in_=k_words[0].rearrange("g t r -> g (t r)").bitcast(I32))
+        nc.sync.dma_start(voffs_sb[:], voffs)
 
         nc.vector.memset(ks_pool[0:KS_ROW, :].bitcast(I32), 0)
         make_identity(nc, ident[:])
@@ -72,25 +74,24 @@ def tile_attend_pkv4q_sigm_kernel(
                 in_=q_rows[4 * quad : 4 * quad + 4],
             )
 
+        def load_queries(b, tile):
+            nc.sync.dma_start(
+                out=tile[:].rearrange("g (o q) -> g o q", q=NQ),
+                in_=q_words[b].rearrange("o g q r -> g o (q r)").bitcast(I32),
+            )
 
-        nc.sync.dma_start(
-            out=qw[:].rearrange("g (c q) -> g c q", q=NQ),
-            in_=q_words.rearrange("b o g q r -> g (b o) (q r)").bitcast(I32),
-        )
-        nc.sync.dma_start(voffs_sb[:], voffs)
+        load_queries(0, qw_first)
         nc.vector.tensor_copy(ks_got[:], ks_pool[:].indirect(offs_sb[:]))
         for o in range(PASSES):
-            for quad in range(4):
-                row = KS_ROW + 16 * o + 4 * quad
+            for j in range(4):
+                row = KS_ROW + 16 * o + j
                 nc.sync.dma_start(
-                    out=ks_plane[o][32 * quad : 32 * quad + 4, :].bitcast(I32),
-                    in_=ks_got[row : row + 4, :].bitcast(I32),
+                    out=ks_plane[o][j:P:32, :].bitcast(I32),
+                    in_=ks_got[row : row + 13 : 4, :].bitcast(I32),
                 )
-        vw_pool = reuse.tile([P, POOL_PAGES * DV], I32, name="vw_pool", align_bytes=64, offset=VW_AT)
-        nc.sync.dma_start(
-            out=vw_pool[:].rearrange("g (u e) -> g u e", e=DV),
-            in_=v_words.rearrange("u g e r -> g u (e r)").bitcast(I32),
-        )
+        qw_late = reuse.tile([P, PASSES * NQ], I32, name="qw_late", align_bytes=64, offset=QW_LATE_AT)
+        load_queries(1, qw_late)
+        qw = [qw_first, qw_late]
         vsc_pool = reuse.tile([P, POOL_PAGES * DV], U8, name="vsc_pool", align_bytes=64, offset=VSC_AT)
         nc.gpsimd.memset(vsc_pool[:].bitcast(I32), 0)
         for quad in range(4):
@@ -98,6 +99,11 @@ def tile_attend_pkv4q_sigm_kernel(
                 out=vsc_pool[32 * quad : 32 * quad + 4, :].bitcast(I32).rearrange("f (u e) -> f u e", u=POOL_PAGES),
                 in_=v_rows[4 * quad : 4 * quad + 4],
             )
+        vw_pool = reuse.tile([P, POOL_PAGES * DV], I32, name="vw_pool", align_bytes=64, offset=VW_AT)
+        nc.sync.dma_start(
+            out=vw_pool[:].rearrange("g (u e) -> g u e", e=DV),
+            in_=v_words.rearrange("u g e r -> g u (e r)").bitcast(I32),
+        )
 
         dealt = vs_pool[:].rearrange("p (u r n h j) -> p r h u n j", u=POOL_PAGES, r=PACK, h=2, j=PACK)
         for r in range(PACK):
@@ -112,8 +118,8 @@ def tile_attend_pkv4q_sigm_kernel(
             reuse.tile([P, PAGE], U32, name=f"kw_got{e}", align_bytes=64, offset=(e % 2) * SLOT_BYTES)
             for e in range(PAGES)
         ]
-        vw_got = reuse.tile([P, PAGES * DV], U32, name="vw_got", align_bytes=64, offset=HALF_AT)
-        vsc_got = reuse.tile([P, PAGES * DV], U8, name="vsc_got", align_bytes=64, offset=POOL_AT + SLOT_BYTES)
+        vw_got = reuse.tile([P, PAGES * DV], U32, name="vw_got", align_bytes=64, offset=POOL_AT + SLOT_BYTES)
+        vsc_got = reuse.tile([P, PAGES * DV], U8, name="vsc_got", align_bytes=64, offset=HALF_AT)
         w_f32 = [
             reuse.tile([P, PAGE], F32, name=f"w_f32{e}", align_bytes=64, offset=e * SLOT_BYTES)
             if e < 2
@@ -150,7 +156,7 @@ def tile_attend_pkv4q_sigm_kernel(
                 q_cols = slice((b * PASSES + o) * NQ, (b * PASSES + o + 1) * NQ)
                 nc.tensor.matmul_mx(
                     out=score[e][:],
-                    lhsT=qw[:, q_cols].bitcast(FP8X4),
+                    lhsT=qw[b][:, o * NQ : (o + 1) * NQ].bitcast(FP8X4),
                     lhsT_scale=qsc[:, q_cols],
                     rhs=kw_part[e][:, o, :].bitcast(FP4X4),
                     rhs_scale=ks_plane[o][:, e * PAGE : (e + 1) * PAGE],
@@ -216,8 +222,8 @@ def tile_attend_pkv4q_sigm_kernel(
         for e in range(PAGES):
             weigh(e)
             turn(e)
-        nc.vector.tensor_copy(vw_got[:], vw_pool[:].bitcast(U32).indirect(voffs_sb[:]))
         nc.vector.tensor_copy(vsc_got[:], vsc_pool[:].indirect(voffs_sb[:]))
+        nc.vector.tensor_copy(vw_got[:], vw_pool[:].bitcast(U32).indirect(voffs_sb[:]))
         quantise(0, 1)
         mix(0)
         mix(1)

@@ -10,17 +10,22 @@ PACK = 4
 PAGES = B * N // PAGE
 POOL_PAGES = T // PAGE
 PASSES = D // 512
-SLOT_BYTES = 4 * PAGE
-KS_AT = SLOT_BYTES - 512
-VSC_AT = 2 * SLOT_BYTES
-QW_LATE_AT = VSC_AT + POOL_PAGES * DV
-VW_AT = QW_LATE_AT + 4 * PASSES * NQ
-POOL_AT = VW_AT + 4 * POOL_PAGES * DV
-LAST_AT = POOL_AT + 4 * T
-HALF_AT = LAST_AT + SLOT_BYTES
+SCALE_ROWS = 16
+QUAD = 32
 FOLD = T // P
-KS_ROW = 96
+KS_ROW = P - PASSES * SCALE_ROWS
 FLOPS = 2 * B * NQ * N * (D + DV)
+
+PAGE_BYTES = 4 * PAGE
+KS_AT = 2 * PAGE_BYTES
+VSC_AT = KS_AT
+QW_LATE_AT = VSC_AT + POOL_PAGES * DV
+VW_AT = KS_AT + T
+VS_AT = VW_AT + 4 * POOL_PAGES * DV
+LAST_AT = VS_AT + 4 * T
+PIECE_AT = LAST_AT + PAGE_BYTES
+
+PIECES = [(e, 0, PACK) for e in range(PAGES - 1)] + [(PAGES - 1, 0, 2), (PAGES - 1, 2, 1), (PAGES - 1, 3, 1)]
 
 F32 = mybir.dt.float32
 BF16 = mybir.dt.bfloat16
@@ -47,15 +52,15 @@ def tile_attend_pkv4q_sigm_kernel(
         voffs_sb = keep.tile([P, PAGES * DV // 16], U16, name="voffs_sb")
         kw_pool = keep.tile([P, T], I32, name="kw_pool", align_bytes=64)
         ks_pool = reuse.tile([P, T], U8, name="ks_pool", align_bytes=64, offset=KS_AT)
-        vs_pool = reuse.tile([P, T], F32, name="vs_pool", align_bytes=64, offset=POOL_AT)
+        vs_pool = reuse.tile([P, T], F32, name="vs_pool", align_bytes=64, offset=VS_AT)
         qw_first = keep.tile([P, PASSES * NQ], I32, name="qw_first", align_bytes=64)
-        qsc = keep.tile([P, B * PASSES * NQ], U8, name="qsc", align_bytes=64)
+        q_plane = keep.tile([P, B * PASSES * NQ], U8, name="q_plane", align_bytes=64)
         ks_got = reuse.tile([P, B * N], U8, name="ks_got", align_bytes=64, offset=VW_AT)
         ks_plane = [keep.tile([P, B * N], U8, name=f"ks_plane{o}", align_bytes=64) for o in range(PASSES)]
         vs_fold = keep.tile([P, FOLD], F32, name="vs_fold")
         ident = keep.tile([P, P], F32, name="ident")
 
-        nc.gpsimd.memset(qsc[:].bitcast(I32), 0)
+        nc.gpsimd.memset(q_plane[:].bitcast(I32), 0)
         nc.sync.dma_start(out=ks_pool[KS_ROW:P, :].bitcast(I32), in_=k_scales.rearrange("o f t -> (o f) t").bitcast(I32))
         nc.sync.dma_start(offs_sb[:], offs)
         nc.sync.dma_start(out=vs_fold[:], in_=vs[0:1].rearrange("a (n m) -> (a n) m", m=FOLD))
@@ -66,13 +71,13 @@ def tile_attend_pkv4q_sigm_kernel(
         make_identity(nc, ident[:])
         for o in range(PASSES):
             nc.gpsimd.memset(ks_plane[o][:].bitcast(I32), 0)
-        q_rows = q_scales.rearrange("b o f q -> f (b o) q").bitcast(I32)
-        v_rows = v_scales.rearrange("u f e -> f u e").bitcast(I32)
-        for quad in range(4):
-            nc.sync.dma_start(
-                out=qsc[32 * quad : 32 * quad + 4, :].bitcast(I32).rearrange("f (c q) -> f c q", c=B * PASSES),
-                in_=q_rows[4 * quad : 4 * quad + 4],
-            )
+
+        def load_scale_rows(tile, rows):
+            for quad in range(P // QUAD):
+                nc.sync.dma_start(
+                    out=tile[QUAD * quad : QUAD * quad + PACK, :].bitcast(I32).rearrange("f (c x) -> f c x", c=rows.shape[1]),
+                    in_=rows[PACK * quad : PACK * (quad + 1)],
+                )
 
         def load_queries(b, tile):
             nc.sync.dma_start(
@@ -80,25 +85,24 @@ def tile_attend_pkv4q_sigm_kernel(
                 in_=q_words[b].rearrange("o g q r -> g o (q r)").bitcast(I32),
             )
 
+        load_scale_rows(q_plane, q_scales.rearrange("b o f q -> f (b o) q").bitcast(I32))
         load_queries(0, qw_first)
+
         nc.vector.tensor_copy(ks_got[:], ks_pool[:].indirect(offs_sb[:]))
         for o in range(PASSES):
-            for j in range(4):
-                row = KS_ROW + 16 * o + j
+            for j in range(PACK):
+                pass_row = KS_ROW + SCALE_ROWS * o
                 nc.sync.dma_start(
-                    out=ks_plane[o][j:P:32, :].bitcast(I32),
-                    in_=ks_got[row : row + 13 : 4, :].bitcast(I32),
+                    out=ks_plane[o][j:P:QUAD, :].bitcast(I32),
+                    in_=ks_got[pass_row + j : pass_row + SCALE_ROWS : PACK, :].bitcast(I32),
                 )
+
         qw_late = reuse.tile([P, PASSES * NQ], I32, name="qw_late", align_bytes=64, offset=QW_LATE_AT)
         load_queries(1, qw_late)
         qw = [qw_first, qw_late]
         vsc_pool = reuse.tile([P, POOL_PAGES * DV], U8, name="vsc_pool", align_bytes=64, offset=VSC_AT)
         nc.gpsimd.memset(vsc_pool[:].bitcast(I32), 0)
-        for quad in range(4):
-            nc.sync.dma_start(
-                out=vsc_pool[32 * quad : 32 * quad + 4, :].bitcast(I32).rearrange("f (u e) -> f u e", u=POOL_PAGES),
-                in_=v_rows[4 * quad : 4 * quad + 4],
-            )
+        load_scale_rows(vsc_pool, v_scales.rearrange("u f e -> f u e").bitcast(I32))
         vw_pool = reuse.tile([P, POOL_PAGES * DV], I32, name="vw_pool", align_bytes=64, offset=VW_AT)
         nc.sync.dma_start(
             out=vw_pool[:].rearrange("g (u e) -> g u e", e=DV),
@@ -115,33 +119,34 @@ def tile_attend_pkv4q_sigm_kernel(
                 nc.scalar.copy(out=dealt[:, r, h], in_=spread[:].rearrange("p j (u n) -> p u n j", u=POOL_PAGES))
 
         kw_got = [
-            reuse.tile([P, PAGE], U32, name=f"kw_got{e}", align_bytes=64, offset=(e % 2) * SLOT_BYTES)
+            reuse.tile([P, PAGE], U32, name=f"kw_got{e}", align_bytes=64, offset=(e % 2) * PAGE_BYTES)
             for e in range(PAGES)
         ]
-        vw_got = reuse.tile([P, PAGES * DV], U32, name="vw_got", align_bytes=64, offset=POOL_AT + SLOT_BYTES)
-        vsc_got = reuse.tile([P, PAGES * DV], U8, name="vsc_got", align_bytes=64, offset=HALF_AT)
+        vw_got = reuse.tile([P, PAGES * DV], U32, name="vw_got", align_bytes=64, offset=VS_AT + PAGE_BYTES)
+        v_plane = reuse.tile([P, PAGES * DV], U8, name="v_plane", align_bytes=64, offset=PIECE_AT)
+        w_at = {0: 0, 1: PAGE_BYTES, PAGES - 1: LAST_AT}
         w_f32 = [
-            reuse.tile([P, PAGE], F32, name=f"w_f32{e}", align_bytes=64, offset=e * SLOT_BYTES)
-            if e < 2
-            else reuse.tile([P, PAGE], F32, name=f"w_f32{e}", align_bytes=64, offset=LAST_AT)
-            if e == PAGES - 1
+            reuse.tile([P, PAGE], F32, name=f"w_f32{e}", align_bytes=64, offset=w_at[e])
+            if e in w_at
             else keep.tile([P, PAGE], F32, name=f"w_f32{e}", align_bytes=64)
             for e in range(PAGES)
         ]
         kw_part = [keep.tile([P, PASSES, PAGE], U16, name=f"kw_part{e}", align_bytes=64) for e in range(PAGES)]
-        pieces = [(e, 0, PACK) for e in range(PAGES - 1)] + [(PAGES - 1, r0, PACK // 2) for r0 in (0, PACK // 2)]
         p_sb = {
-            (e, r0): reuse.tile([P, count * P], F32, name=f"p_sb{e}_{r0}", align_bytes=64, offset=HALF_AT)
+            (e, r0): reuse.tile([P, places * P], F32, name=f"p_sb{e}_{r0}", align_bytes=64, offset=PIECE_AT)
             if (e, r0) == (PAGES - 1, 0)
-            else keep.tile([P, count * P], F32, name=f"p_sb{e}_{r0}", align_bytes=64)
-            for e, r0, count in pieces
+            else keep.tile([P, places * P], F32, name=f"p_sb{e}_{r0}", align_bytes=64)
+            for e, r0, places in PIECES
         }
         w_bf = keep.tile([P, PAGES, NQ * PACK], BF16, name="w_bf", align_bytes=64)
         w_codes = reuse.tile([P, PAGES * NQ], U32, name="w_codes", align_bytes=64, offset=LAST_AT)
-        w_scale = keep.tile([P, PAGES * NQ], U8, name="w_scale", align_bytes=64)
+        w_plane = keep.tile([P, PAGES * NQ], U8, name="w_plane", align_bytes=64)
         score = [psum.tile([P, PAGE], F32, name=f"score{e}", tag=f"score{e % 2}") for e in range(PAGES)]
         w_turn = [psum.tile([P, PACK, P], F32, name=f"w_turn{e}", tag=f"turn{e}") for e in range(PAGES)]
         y_ps = [psum.tile([P, DV], F32, name=f"y_ps{b}", tag=f"y{b}") for b in range(B)]
+
+        def pieces_of(e):
+            return [(r0, places) for page, r0, places in PIECES if page == e]
 
         def gather_keys(e):
             cols = slice(e * PAGE // 16, (e + 1) * PAGE // 16)
@@ -153,30 +158,27 @@ def tile_attend_pkv4q_sigm_kernel(
         def scores(e):
             b = e * PAGE // N
             for o in range(PASSES):
-                q_cols = slice((b * PASSES + o) * NQ, (b * PASSES + o + 1) * NQ)
                 nc.tensor.matmul_mx(
                     out=score[e][:],
                     lhsT=qw[b][:, o * NQ : (o + 1) * NQ].bitcast(FP8X4),
-                    lhsT_scale=qsc[:, q_cols],
+                    lhsT_scale=q_plane[:, (b * PASSES + o) * NQ : (b * PASSES + o + 1) * NQ],
                     rhs=kw_part[e][:, o, :].bitcast(FP4X4),
                     rhs_scale=ks_plane[o][:, e * PAGE : (e + 1) * PAGE],
                     start=(o == 0),
                     stop=(o == PASSES - 1),
                 )
-            step = PACK // 2 if e == PAGES - 1 else PACK
-            for r0 in range(0, PACK, step):
+            for r0, places in pieces_of(e):
                 nc.scalar.activation(
-                    out=p_sb[e, r0][:].rearrange("q (r s) -> q r s", r=step),
-                    in_=score[e][:].rearrange("q (s r) -> q r s", r=PACK)[:, r0 : r0 + step, :],
+                    out=p_sb[e, r0][:].rearrange("q (r s) -> q r s", r=places),
+                    in_=score[e][:].rearrange("q (s r) -> q r s", r=PACK)[:, r0 : r0 + places, :],
                     func=ACT.Sigmoid,
                 )
 
         def weigh(e):
-            step = PAGE // 2 if e == PAGES - 1 else PAGE
-            for s0 in range(0, PAGE, step):
-                cols = slice((e * PAGE + s0) // 16, (e * PAGE + s0 + step) // 16)
-                slots = slice(s0, s0 + step)
-                nc.vector.tensor_tensor(w_f32[e][:, slots], vs_pool[:].indirect(offs_sb[:, cols]), p_sb[e, s0 // P][:], MULT)
+            for r0, places in pieces_of(e):
+                first, last = r0 * P, (r0 + places) * P
+                cols = slice((e * PAGE + first) // 16, (e * PAGE + last) // 16)
+                nc.vector.tensor_tensor(w_f32[e][:, first:last], vs_pool[:].indirect(offs_sb[:, cols]), p_sb[e, r0][:], MULT)
 
         def turn(e):
             for r in range(PACK):
@@ -190,21 +192,21 @@ def tile_attend_pkv4q_sigm_kernel(
             cols = slice(first * NQ, (last + 1) * NQ)
             nc.vector.quantize_mx(
                 out=w_codes[:, cols].bitcast(FP8X4),
-                scales=w_scale[:, cols],
-                in_=w_bf[:, first : last + 1, :].rearrange("m e c -> m (e c)"),
+                scales=w_plane[:, cols],
+                in_=w_bf[:, first : last + 1, :].rearrange("s e c -> s (e c)"),
             )
 
         def mix(e):
-            b, first = divmod(e, N // PAGE)
+            b, page_in_b = divmod(e, N // PAGE)
             v_cols = slice(e * DV, (e + 1) * DV)
             nc.tensor.matmul_mx(
                 out=y_ps[b][:],
                 lhsT=w_codes[:, e * NQ : (e + 1) * NQ].bitcast(FP8X4),
-                lhsT_scale=w_scale[:, e * NQ : (e + 1) * NQ],
+                lhsT_scale=w_plane[:, e * NQ : (e + 1) * NQ],
                 rhs=vw_got[:, v_cols].bitcast(FP8X4),
-                rhs_scale=vsc_got[:, v_cols],
-                start=(first == 0),
-                stop=(first == N // PAGE - 1),
+                rhs_scale=v_plane[:, v_cols],
+                start=(page_in_b == 0),
+                stop=(page_in_b == N // PAGE - 1),
             )
 
         def store(b):
@@ -222,14 +224,13 @@ def tile_attend_pkv4q_sigm_kernel(
         for e in range(PAGES):
             weigh(e)
             turn(e)
-        nc.vector.tensor_copy(vsc_got[:], vsc_pool[:].indirect(voffs_sb[:]))
+        nc.vector.tensor_copy(v_plane[:], vsc_pool[:].indirect(voffs_sb[:]))
         nc.vector.tensor_copy(vw_got[:], vw_pool[:].bitcast(U32).indirect(voffs_sb[:]))
         quantise(0, 1)
         mix(0)
         mix(1)
         store(0)
-        quantise(2, 2)
-        mix(2)
-        quantise(3, 3)
-        mix(3)
+        for e in (PAGES - 2, PAGES - 1):
+            quantise(e, e)
+            mix(e)
         store(1)

@@ -25,7 +25,7 @@ VS_AT = VW_AT + 4 * POOL_PAGES * DV
 LAST_AT = VS_AT + 4 * T
 PIECE_AT = LAST_AT + PAGE_BYTES
 
-PIECES = [(e, 0, PACK) for e in range(PAGES - 1)] + [(PAGES - 1, 0, 2), (PAGES - 1, 2, 1), (PAGES - 1, 3, 1)]
+PIECES = [(e, 0, PACK) for e in range(PAGES - 1)] + [(PAGES - 1, 0, 2), (PAGES - 1, 2, 2)]
 
 F32 = mybir.dt.float32
 BF16 = mybir.dt.bfloat16
@@ -211,7 +211,10 @@ def tile_attend_pkv4q_sigm_kernel(
 
         def store(b):
             y_sb = keep.tile([P, DV], F32, name=f"y_sb{b}")
-            nc.scalar.activation(out=y_sb[:], in_=y_ps[b][:], func=ACT.Copy, scale=1.0 / 16.0)
+            if b == 0:
+                nc.scalar.activation(out=y_sb[:], in_=y_ps[b][:], func=ACT.Copy, scale=1.0 / 16.0)
+            else:
+                nc.vector.tensor_scalar_mul(y_sb[:], y_ps[b][:], 1.0 / 16.0)
             nc.sync.dma_start(out=out[b], in_=y_sb[:])
 
         for pair in range(0, PAGES, 2):

@@ -18,12 +18,12 @@ FLOPS = 2 * B * NQ * N * (D + DV)
 
 PAGE_BYTES = 4 * PAGE
 KS_AT = 2 * PAGE_BYTES
-VSC_AT = KS_AT
-QW_LATE_AT = VSC_AT + POOL_PAGES * DV
-VW_AT = KS_AT + T
-VS_AT = VW_AT + 4 * POOL_PAGES * DV
-LAST_AT = VS_AT + 4 * T
+QW_LATE_AT = KS_AT
+KS_GOT_AT = KS_AT + T
+VW_AT = KS_GOT_AT + PAGES * DV
+LAST_AT = VW_AT + 4 * POOL_PAGES * DV
 PIECE_AT = LAST_AT + PAGE_BYTES
+VSC_ROW = P - SCALE_ROWS
 
 PIECES = [(e, 0, PACK) for e in range(PAGES - 1)] + [(PAGES - 1, 0, 2), (PAGES - 1, 2, 2)]
 
@@ -52,22 +52,30 @@ def tile_attend_pkv4q_sigm_kernel(
         voffs_sb = keep.tile([P, PAGES * DV // 16], U16, name="voffs_sb")
         kw_pool = keep.tile([P, T], I32, name="kw_pool", align_bytes=64)
         ks_pool = reuse.tile([P, T], U8, name="ks_pool", align_bytes=64, offset=KS_AT)
-        vs_pool = reuse.tile([P, T], F32, name="vs_pool", align_bytes=64, offset=VS_AT)
+        vs_pool = keep.tile([P, T], F32, name="vs_pool", align_bytes=64)
+        vsc_pool = keep.tile([P, POOL_PAGES * DV], U8, name="vsc_pool", align_bytes=64)
+        vsc_got = keep.tile([P, PAGES * DV], U8, name="vsc_got", align_bytes=64)
         qw_first = keep.tile([P, PASSES * NQ], I32, name="qw_first", align_bytes=64)
         q_plane = keep.tile([P, B * PASSES * NQ], U8, name="q_plane", align_bytes=64)
-        ks_got = reuse.tile([P, B * N], U8, name="ks_got", align_bytes=64, offset=VW_AT)
+        ks_got = reuse.tile([P, B * N], U8, name="ks_got", align_bytes=64, offset=KS_GOT_AT)
         ks_plane = [keep.tile([P, B * N], U8, name=f"ks_plane{o}", align_bytes=64) for o in range(PASSES)]
         vs_fold = keep.tile([P, FOLD], F32, name="vs_fold")
         ident = keep.tile([P, P], F32, name="ident")
 
         nc.gpsimd.memset(q_plane[:].bitcast(I32), 0)
-        nc.sync.dma_start(out=ks_pool[KS_ROW:P, :].bitcast(I32), in_=k_scales.rearrange("o f t -> (o f) t").bitcast(I32))
         nc.sync.dma_start(offs_sb[:], offs)
-        nc.sync.dma_start(out=vs_fold[:], in_=vs[0:1].rearrange("a (n m) -> (a n) m", m=FOLD))
-        nc.sync.dma_start(out=kw_pool[:], in_=k_words[0].rearrange("g t r -> g (t r)").bitcast(I32))
+        nc.scalar.dma_start(out=vs_fold[:], in_=vs[0:1].rearrange("a (n m) -> (a n) m", m=FOLD))
         nc.sync.dma_start(voffs_sb[:], voffs)
+        nc.scalar.dma_start(out=ks_pool[KS_ROW:P, :].bitcast(I32), in_=k_scales.rearrange("o f t -> (o f) t").bitcast(I32))
+        kw_rows = k_words[0].rearrange("g t r -> g (t r)").bitcast(I32)
+        nc.sync.dma_start(out=kw_pool[:, 0 : T // 2], in_=kw_rows[:, 0 : T // 2])
+        nc.scalar.dma_start(
+            out=vsc_pool[VSC_ROW:P, :].bitcast(I32).rearrange("f (u x) -> f u x", u=POOL_PAGES),
+            in_=v_scales.rearrange("u f e -> f u e").bitcast(I32),
+        )
 
         nc.vector.memset(ks_pool[0:KS_ROW, :].bitcast(I32), 0)
+        nc.vector.memset(vsc_pool[0:VSC_ROW, :].bitcast(I32), 0)
         make_identity(nc, ident[:])
         for o in range(PASSES):
             nc.gpsimd.memset(ks_plane[o][:].bitcast(I32), 0)
@@ -86,6 +94,7 @@ def tile_attend_pkv4q_sigm_kernel(
             )
 
         load_scale_rows(q_plane, q_scales.rearrange("b o f q -> f (b o) q").bitcast(I32))
+        nc.sync.dma_start(out=kw_pool[:, T // 2 : T], in_=kw_rows[:, T // 2 : T])
         load_queries(0, qw_first)
 
         nc.vector.tensor_copy(ks_got[:], ks_pool[:].indirect(offs_sb[:]))
@@ -100,14 +109,15 @@ def tile_attend_pkv4q_sigm_kernel(
         qw_late = reuse.tile([P, PASSES * NQ], I32, name="qw_late", align_bytes=64, offset=QW_LATE_AT)
         load_queries(1, qw_late)
         qw = [qw_first, qw_late]
-        vsc_pool = reuse.tile([P, POOL_PAGES * DV], U8, name="vsc_pool", align_bytes=64, offset=VSC_AT)
-        nc.gpsimd.memset(vsc_pool[:].bitcast(I32), 0)
-        load_scale_rows(vsc_pool, v_scales.rearrange("u f e -> f u e").bitcast(I32))
+        nc.vector.tensor_copy(vsc_got[:], vsc_pool[:].indirect(voffs_sb[:]))
         vw_pool = reuse.tile([P, POOL_PAGES * DV], I32, name="vw_pool", align_bytes=64, offset=VW_AT)
         nc.sync.dma_start(
             out=vw_pool[:].rearrange("g (u e) -> g u e", e=DV),
             in_=v_words.rearrange("u g e r -> g u (e r)").bitcast(I32),
         )
+        v_plane = reuse.tile([P, PAGES * DV], U8, name="v_plane", align_bytes=64, offset=KS_GOT_AT)
+        for j in range(PACK):
+            nc.sync.dma_start(out=v_plane[j:P:QUAD, :].bitcast(I32), in_=vsc_got[VSC_ROW + j : P : PACK, :].bitcast(I32))
 
         dealt = vs_pool[:].rearrange("p (u r n h j) -> p r h u n j", u=POOL_PAGES, r=PACK, h=2, j=PACK)
         for r in range(PACK):
@@ -122,8 +132,7 @@ def tile_attend_pkv4q_sigm_kernel(
             reuse.tile([P, PAGE], U32, name=f"kw_got{e}", align_bytes=64, offset=(e % 2) * PAGE_BYTES)
             for e in range(PAGES)
         ]
-        vw_got = reuse.tile([P, PAGES * DV], U32, name="vw_got", align_bytes=64, offset=VS_AT + PAGE_BYTES)
-        v_plane = reuse.tile([P, PAGES * DV], U8, name="v_plane", align_bytes=64, offset=PIECE_AT)
+        vw_got = reuse.tile([P, PAGES * DV], U32, name="vw_got", align_bytes=64, offset=PIECE_AT)
         w_at = {0: 0, 1: PAGE_BYTES, PAGES - 1: LAST_AT}
         w_f32 = [
             reuse.tile([P, PAGE], F32, name=f"w_f32{e}", align_bytes=64, offset=w_at[e])
@@ -132,9 +141,10 @@ def tile_attend_pkv4q_sigm_kernel(
             for e in range(PAGES)
         ]
         kw_part = [keep.tile([P, PASSES, PAGE], U16, name=f"kw_part{e}", align_bytes=64) for e in range(PAGES)]
+        p_at = {(PAGES - 1, 0): PIECE_AT}
         p_sb = {
-            (e, r0): reuse.tile([P, places * P], F32, name=f"p_sb{e}_{r0}", align_bytes=64, offset=PIECE_AT)
-            if (e, r0) == (PAGES - 1, 0)
+            (e, r0): reuse.tile([P, places * P], F32, name=f"p_sb{e}_{r0}", align_bytes=64, offset=p_at[e, r0])
+            if (e, r0) in p_at
             else keep.tile([P, places * P], F32, name=f"p_sb{e}_{r0}", align_bytes=64)
             for e, r0, places in PIECES
         }
@@ -227,7 +237,6 @@ def tile_attend_pkv4q_sigm_kernel(
         for e in range(PAGES):
             weigh(e)
             turn(e)
-        nc.vector.tensor_copy(v_plane[:], vsc_pool[:].indirect(voffs_sb[:]))
         nc.vector.tensor_copy(vw_got[:], vw_pool[:].bitcast(U32).indirect(voffs_sb[:]))
         quantise(0, 1)
         mix(0)

@@ -62,6 +62,8 @@ def tile_attend_pkv4q_sigm_kernel(
         vs_fold = keep.tile([P, FOLD], F32, name="vs_fold")
         ident = keep.tile([P, P], F32, name="ident")
 
+        warm = keep.tile([P, 16], F32, name="warm")
+        nc.gpsimd.memset(warm[:, 0:8], 0.0)
         nc.gpsimd.memset(q_plane[:].bitcast(I32), 0)
         nc.sync.dma_start(offs_sb[:], offs)
         nc.scalar.dma_start(out=vs_fold[:], in_=vs[0:1].rearrange("a (n m) -> (a n) m", m=FOLD))
@@ -73,6 +75,8 @@ def tile_attend_pkv4q_sigm_kernel(
             out=vsc_pool[VSC_ROW:P, :].bitcast(I32).rearrange("f (u x) -> f u x", u=POOL_PAGES),
             in_=v_scales.rearrange("u f e -> f u e").bitcast(I32),
         )
+
+        nc.scalar.activation(out=warm[:, 8:9], in_=warm[:, 0:1], func=ACT.Sigmoid)
 
         nc.vector.memset(ks_pool[0:KS_ROW, :].bitcast(I32), 0)
         nc.vector.memset(vsc_pool[0:VSC_ROW, :].bitcast(I32), 0)
@@ -133,13 +137,15 @@ def tile_attend_pkv4q_sigm_kernel(
             for e in range(PAGES)
         ]
         vw_got = reuse.tile([P, PAGES * DV], U32, name="vw_got", align_bytes=64, offset=PIECE_AT)
-        w_at = {0: 0, 1: PAGE_BYTES, PAGES - 1: LAST_AT}
+        w_at = {0: 0, 1: PAGE_BYTES}
         w_f32 = [
             reuse.tile([P, PAGE], F32, name=f"w_f32{e}", align_bytes=64, offset=w_at[e])
             if e in w_at
             else keep.tile([P, PAGE], F32, name=f"w_f32{e}", align_bytes=64)
-            for e in range(PAGES)
+            for e in range(PAGES - 1)
         ]
+        vs_last = keep.tile([P, PAGE], F32, name="vs_last", align_bytes=64)
+        w_pairs = reuse.tile([P, 2, 2 * P], BF16, name="w_pairs", align_bytes=64, offset=LAST_AT)
         kw_part = [keep.tile([P, PASSES, PAGE], U16, name=f"kw_part{e}", align_bytes=64) for e in range(PAGES)]
         p_at = {(PAGES - 1, 0): PIECE_AT}
         p_sb = {
@@ -149,7 +155,7 @@ def tile_attend_pkv4q_sigm_kernel(
             for e, r0, places in PIECES
         }
         w_bf = keep.tile([P, PAGES, NQ * PACK], BF16, name="w_bf", align_bytes=64)
-        w_codes = reuse.tile([P, PAGES * NQ], U32, name="w_codes", align_bytes=64, offset=LAST_AT)
+        w_codes = keep.tile([P, PAGES * NQ], U32, name="w_codes", align_bytes=64)
         w_plane = keep.tile([P, PAGES * NQ], U8, name="w_plane", align_bytes=64)
         score = [psum.tile([P, PAGE], F32, name=f"score{e}", tag=f"score{e % 2}") for e in range(PAGES)]
         w_turn = [psum.tile([P, PACK, P], F32, name=f"w_turn{e}", tag=f"turn{e}") for e in range(PAGES)]
@@ -198,6 +204,21 @@ def tile_attend_pkv4q_sigm_kernel(
                 in_=w_turn[e][:].rearrange("s r q -> s q r"),
             )
 
+        def weigh_last():
+            e = PAGES - 1
+            for u, (r0, places) in enumerate(pieces_of(e)):
+                nc.vector.tensor_tensor(
+                    w_pairs[:, u, :].rearrange("q (c i r) -> q c r i", i=PACK, r=places),
+                    p_sb[e, r0][:].rearrange("q (r c i) -> q c r i", i=PACK, r=places),
+                    vs_last[:, r0 * P : (r0 + places) * P].rearrange("q (r c i) -> q c r i", i=PACK, r=places),
+                    MULT,
+                )
+                nc.tensor.transpose(w_turn[e][:, u, :], w_pairs[:, u, :].bitcast(F32), ident[:])
+            nc.scalar.copy(
+                out=w_bf[:, e, :].bitcast(F32).rearrange("s (q u) -> s q u", u=2),
+                in_=w_turn[e][:, 0:2, :].rearrange("s u q -> s q u"),
+            )
+
         def quantise(first, last):
             cols = slice(first * NQ, (last + 1) * NQ)
             nc.vector.quantize_mx(
@@ -227,6 +248,7 @@ def tile_attend_pkv4q_sigm_kernel(
                 nc.vector.tensor_scalar_mul(y_sb[:], y_ps[b][:], 1.0 / 16.0)
             nc.sync.dma_start(out=out[b], in_=y_sb[:])
 
+        nc.scalar.activation(vs_last[:], vs_pool[:].indirect(offs_sb[:, (PAGES - 1) * PAGE // 16 :]), ACT.Copy)
         for pair in range(0, PAGES, 2):
             gather_keys(pair)
             gather_keys(pair + 1)
@@ -234,11 +256,12 @@ def tile_attend_pkv4q_sigm_kernel(
             part_keys(pair + 1)
         for e in range(PAGES):
             scores(e)
-        for e in range(PAGES):
+        for e in range(PAGES - 1):
             weigh(e)
             turn(e)
-        nc.vector.tensor_copy(vw_got[:], vw_pool[:].bitcast(U32).indirect(voffs_sb[:]))
+        weigh_last()
         quantise(0, 1)
+        nc.vector.tensor_copy(vw_got[:], vw_pool[:].bitcast(U32).indirect(voffs_sb[:]))
         mix(0)
         mix(1)
         store(0)

@@ -65,17 +65,15 @@ def tile_attend_pkv4q_sigm_kernel(
         warm = keep.tile([P, 16], F32, name="warm")
         nc.gpsimd.memset(warm[:, 0:8], 0.0)
         nc.gpsimd.memset(q_plane[:].bitcast(I32), 0)
-        nc.sync.dma_start(offs_sb[:], offs)
+        nc.sync.dma_start(out=ks_pool[KS_ROW:P, :].bitcast(I32), in_=k_scales.rearrange("o f t -> (o f) t").bitcast(I32))
         nc.scalar.dma_start(out=vs_fold[:], in_=vs[0:1].rearrange("a (n m) -> (a n) m", m=FOLD))
-        nc.sync.dma_start(voffs_sb[:], voffs)
-        nc.scalar.dma_start(out=ks_pool[KS_ROW:P, :].bitcast(I32), in_=k_scales.rearrange("o f t -> (o f) t").bitcast(I32))
-        kw_rows = k_words[0].rearrange("g t r -> g (t r)").bitcast(I32)
-        nc.sync.dma_start(out=kw_pool[:, 0 : T // 2], in_=kw_rows[:, 0 : T // 2])
+        nc.sync.dma_start(offs_sb[:], offs)
         nc.scalar.dma_start(
             out=vsc_pool[VSC_ROW:P, :].bitcast(I32).rearrange("f (u x) -> f u x", u=POOL_PAGES),
             in_=v_scales.rearrange("u f e -> f u e").bitcast(I32),
         )
-
+        nc.sync.dma_start(voffs_sb[:], voffs)
+        nc.sync.dma_start(out=kw_pool[:], in_=k_words[0].rearrange("g t r -> g (t r)").bitcast(I32))
         nc.scalar.activation(out=warm[:, 8:9], in_=warm[:, 0:1], func=ACT.Sigmoid)
 
         nc.vector.memset(ks_pool[0:KS_ROW, :].bitcast(I32), 0)
@@ -98,7 +96,6 @@ def tile_attend_pkv4q_sigm_kernel(
             )
 
         load_scale_rows(q_plane, q_scales.rearrange("b o f q -> f (b o) q").bitcast(I32))
-        nc.sync.dma_start(out=kw_pool[:, T // 2 : T], in_=kw_rows[:, T // 2 : T])
         load_queries(0, qw_first)
 
         nc.vector.tensor_copy(ks_got[:], ks_pool[:].indirect(offs_sb[:]))

@@ -154,9 +154,9 @@ def tile_attend_pkv4q_sigm_kernel(
         w_bf = keep.tile([P, PAGES, NQ * PACK], BF16, name="w_bf", align_bytes=64)
         w_codes = keep.tile([P, PAGES * NQ], U32, name="w_codes", align_bytes=64)
         w_plane = keep.tile([P, PAGES * NQ], U8, name="w_plane", align_bytes=64)
-        score = [psum.tile([P, PAGE], F32, name=f"score{e}", tag=f"score{e % 2}") for e in range(PAGES)]
+        score = [psum.tile([P, PAGE], F32, name=f"score{e}", tag=f"bank{e}") for e in range(PAGES)]
         w_turn = [psum.tile([P, PACK, P], F32, name=f"w_turn{e}", tag=f"turn{e}") for e in range(PAGES)]
-        y_ps = [psum.tile([P, DV], F32, name=f"y_ps{b}", tag=f"y{b}") for b in range(B)]
+        y_ps = [psum.tile([P, DV], F32, name=f"y_ps{b}", tag=f"bank{b}") for b in range(B)]
 
         def pieces_of(e):
             return [(r0, places) for page, r0, places in PIECES if page == e]
@@ -170,15 +170,16 @@ def tile_attend_pkv4q_sigm_kernel(
 
         def scores(e):
             b = e * PAGE // N
-            for o in range(PASSES):
+            order = range(PASSES) if e == 0 else range(PASSES - 1, -1, -1)
+            for o in order:
                 nc.tensor.matmul_mx(
                     out=score[e][:],
                     lhsT=qw[b][:, o * NQ : (o + 1) * NQ].bitcast(FP8X4),
                     lhsT_scale=q_plane[:, (b * PASSES + o) * NQ : (b * PASSES + o + 1) * NQ],
                     rhs=kw_part[e][:, o, :].bitcast(FP4X4),
                     rhs_scale=ks_plane[o][:, e * PAGE : (e + 1) * PAGE],
-                    start=(o == 0),
-                    stop=(o == PASSES - 1),
+                    start=(o == order[0]),
+                    stop=(o == order[-1]),
                 )
             for r0, places in pieces_of(e):
                 nc.scalar.activation(

@@ -62,8 +62,6 @@ def tile_attend_pkv4q_sigm_kernel(
         vs_fold = keep.tile([P, FOLD], F32, name="vs_fold")
         ident = keep.tile([P, P], F32, name="ident")
 
-        warm = keep.tile([P, 16], F32, name="warm")
-        nc.gpsimd.memset(warm[:, 0:8], 0.0)
         nc.gpsimd.memset(q_plane[:].bitcast(I32), 0)
         nc.sync.dma_start(out=ks_pool[KS_ROW:P, :].bitcast(I32), in_=k_scales.rearrange("o f t -> (o f) t").bitcast(I32))
         nc.scalar.dma_start(out=vs_fold[:], in_=vs[0:1].rearrange("a (n m) -> (a n) m", m=FOLD))
@@ -74,7 +72,6 @@ def tile_attend_pkv4q_sigm_kernel(
         )
         nc.sync.dma_start(voffs_sb[:], voffs)
         nc.sync.dma_start(out=kw_pool[:], in_=k_words[0].rearrange("g t r -> g (t r)").bitcast(I32))
-        nc.scalar.activation(out=warm[:, 8:9], in_=warm[:, 0:1], func=ACT.Sigmoid)
 
         nc.vector.memset(ks_pool[0:KS_ROW, :].bitcast(I32), 0)
         nc.vector.memset(vsc_pool[0:VSC_ROW, :].bitcast(I32), 0)

@@ -12,20 +12,19 @@ POOL_PAGES = T // PAGE
 PASSES = D // 512
 SCALE_ROWS = 16
 QUAD = 32
-FOLD = T // P
+QUADS = P // QUAD
 KS_ROW = P - PASSES * SCALE_ROWS
+VSC_ROW = P - SCALE_ROWS
+VS_ROW = P - POOL_PAGES
 FLOPS = 2 * B * NQ * N * (D + DV)
 
-PAGE_BYTES = 4 * PAGE
-KS_AT = 2 * PAGE_BYTES
-QW_LATE_AT = KS_AT
+KS_AT = 0
 KS_GOT_AT = KS_AT + T
-VW_AT = KS_GOT_AT + PAGES * DV
-LAST_AT = VW_AT + 4 * POOL_PAGES * DV
-PIECE_AT = LAST_AT + PAGE_BYTES
-VSC_ROW = P - SCALE_ROWS
-
-PIECES = [(e, 0, PACK) for e in range(PAGES - 1)] + [(PAGES - 1, 0, 2), (PAGES - 1, 2, 2)]
+VSC_GOT_AT = KS_GOT_AT
+QW_LATE_AT = VSC_GOT_AT + PAGES * DV
+VW_AT = QW_LATE_AT + 4 * PASSES * NQ
+PART_AT = VW_AT + 4 * POOL_PAGES * DV
+PART_BYTES = 2 * PASSES * PAGE
 
 F32 = mybir.dt.float32
 BF16 = mybir.dt.bfloat16
@@ -52,39 +51,33 @@ def tile_attend_pkv4q_sigm_kernel(
         voffs_sb = keep.tile([P, PAGES * DV // 16], U16, name="voffs_sb")
         kw_pool = keep.tile([P, T], I32, name="kw_pool", align_bytes=64)
         ks_pool = reuse.tile([P, T], U8, name="ks_pool", align_bytes=64, offset=KS_AT)
+        ks_got = [
+            reuse.tile([P, N], U8, name=f"ks_got{b}", align_bytes=64, offset=KS_GOT_AT + b * N) for b in range(B)
+        ]
+        ks_dealt = keep.tile([P, B * N], U8, name="ks_dealt", align_bytes=64)
+        vs_rows = keep.tile([P, PAGE], F32, name="vs_rows", align_bytes=64)
+        vs_cols = keep.tile([P, POOL_PAGES, PACK], F32, name="vs_cols", align_bytes=64)
         vs_pool = keep.tile([P, T], F32, name="vs_pool", align_bytes=64)
         vsc_pool = keep.tile([P, POOL_PAGES * DV], U8, name="vsc_pool", align_bytes=64)
-        vsc_got = keep.tile([P, PAGES * DV], U8, name="vsc_got", align_bytes=64)
+        v_plane = keep.tile([P, PAGES * DV], U8, name="v_plane", align_bytes=64)
         qw_first = keep.tile([P, PASSES * NQ], I32, name="qw_first", align_bytes=64)
+        qs_rows = keep.tile([PACK, B * PASSES, QUADS, NQ // 4], I32, name="qs_rows", align_bytes=64)
         q_plane = keep.tile([P, B * PASSES * NQ], U8, name="q_plane", align_bytes=64)
-        ks_got = reuse.tile([P, B * N], U8, name="ks_got", align_bytes=64, offset=KS_GOT_AT)
-        ks_plane = [keep.tile([P, B * N], U8, name=f"ks_plane{o}", align_bytes=64) for o in range(PASSES)]
-        vs_fold = keep.tile([P, FOLD], F32, name="vs_fold")
         ident = keep.tile([P, P], F32, name="ident")
 
-        nc.gpsimd.memset(q_plane[:].bitcast(I32), 0)
-        nc.sync.dma_start(out=ks_pool[KS_ROW:P, :].bitcast(I32), in_=k_scales.rearrange("o f t -> (o f) t").bitcast(I32))
-        nc.scalar.dma_start(out=vs_fold[:], in_=vs[0:1].rearrange("a (n m) -> (a n) m", m=FOLD))
+        nc.sync.dma_start(out=ks_pool[KS_ROW:P, :].bitcast(I32), in_=k_scales.rearrange("o f t -> f o t").bitcast(I32))
+        nc.scalar.dma_start(
+            out=qs_rows[:].rearrange("j c u x -> j (c u) x"),
+            in_=q_scales.rearrange("b o (u j) q -> j (b o u) q", j=PACK).bitcast(I32),
+        )
         nc.sync.dma_start(offs_sb[:], offs)
+        nc.scalar.dma_start(out=vs_rows[VS_ROW:P, :], in_=vs[0:1].rearrange("a (u m) -> (a u) m", m=PAGE))
+        nc.sync.dma_start(voffs_sb[:], voffs)
         nc.scalar.dma_start(
             out=vsc_pool[VSC_ROW:P, :].bitcast(I32).rearrange("f (u x) -> f u x", u=POOL_PAGES),
             in_=v_scales.rearrange("u f e -> f u e").bitcast(I32),
         )
-        nc.sync.dma_start(voffs_sb[:], voffs)
         nc.sync.dma_start(out=kw_pool[:], in_=k_words[0].rearrange("g t r -> g (t r)").bitcast(I32))
-
-        nc.vector.memset(ks_pool[0:KS_ROW, :].bitcast(I32), 0)
-        nc.vector.memset(vsc_pool[0:VSC_ROW, :].bitcast(I32), 0)
-        make_identity(nc, ident[:])
-        for o in range(PASSES):
-            nc.gpsimd.memset(ks_plane[o][:].bitcast(I32), 0)
-
-        def load_scale_rows(tile, rows):
-            for quad in range(P // QUAD):
-                nc.sync.dma_start(
-                    out=tile[QUAD * quad : QUAD * quad + PACK, :].bitcast(I32).rearrange("f (c x) -> f c x", c=rows.shape[1]),
-                    in_=rows[PACK * quad : PACK * (quad + 1)],
-                )
 
         def load_queries(b, tile):
             nc.sync.dma_start(
@@ -92,138 +85,120 @@ def tile_attend_pkv4q_sigm_kernel(
                 in_=q_words[b].rearrange("o g q r -> g o (q r)").bitcast(I32),
             )
 
-        load_scale_rows(q_plane, q_scales.rearrange("b o f q -> f (b o) q").bitcast(I32))
         load_queries(0, qw_first)
 
-        nc.vector.tensor_copy(ks_got[:], ks_pool[:].indirect(offs_sb[:]))
-        for o in range(PASSES):
-            for j in range(PACK):
-                pass_row = KS_ROW + SCALE_ROWS * o
-                nc.sync.dma_start(
-                    out=ks_plane[o][j:P:QUAD, :].bitcast(I32),
-                    in_=ks_got[pass_row + j : pass_row + SCALE_ROWS : PACK, :].bitcast(I32),
-                )
+        nc.gpsimd.memset(vs_rows[0:VS_ROW, :], 0.0)
+        make_identity(nc, ident[:])
+        nc.gpsimd.memset(v_plane[:].bitcast(I32), 0)
+        nc.vector.memset(q_plane[:].bitcast(I32), 0)
+        nc.vector.memset(ks_pool[0:KS_ROW, :].bitcast(I32), 0)
+        nc.vector.memset(vsc_pool[0:VSC_ROW, :].bitcast(I32), 0)
 
+        for quad in range(QUADS):
+            nc.vector.tensor_copy(
+                q_plane[QUAD * quad : QUAD * quad + PACK, :].bitcast(I32).rearrange("j (c x) -> j c x", c=B * PASSES),
+                qs_rows[:, :, quad, :],
+            )
+
+        for b in range(B):
+            nc.vector.tensor_copy(ks_got[b][:], ks_pool[:].indirect(offs_sb[:, b * N // 16 : (b + 1) * N // 16]))
+        for b in range(B):
+            nc.vector.tensor_copy(
+                ks_dealt[:, b * N : (b + 1) * N].rearrange("f (e h r s) -> f e h s r", e=N // PAGE, h=2, r=2),
+                ks_got[b][:].rearrange("f (e s h r) -> f e h s r", e=N // PAGE, h=2, r=2),
+            )
+        ks_plane = reuse.tile([P, PASSES, B * N], U8, name="ks_plane", align_bytes=64, offset=KS_AT)
+        for quad in (0, 2, 1, 3):
+            first = KS_ROW + PASSES * PACK * quad
+            nc.sync.dma_start(
+                out=ks_plane[QUAD * quad : QUAD * quad + PACK].bitcast(I32),
+                in_=ks_dealt[first : first + PASSES * PACK, :].bitcast(I32),
+            )
         qw_late = reuse.tile([P, PASSES * NQ], I32, name="qw_late", align_bytes=64, offset=QW_LATE_AT)
         load_queries(1, qw_late)
         qw = [qw_first, qw_late]
-        nc.vector.tensor_copy(vsc_got[:], vsc_pool[:].indirect(voffs_sb[:]))
         vw_pool = reuse.tile([P, POOL_PAGES * DV], I32, name="vw_pool", align_bytes=64, offset=VW_AT)
         nc.sync.dma_start(
             out=vw_pool[:].rearrange("g (u e) -> g u e", e=DV),
             in_=v_words.rearrange("u g e r -> g u (e r)").bitcast(I32),
         )
-        v_plane = reuse.tile([P, PAGES * DV], U8, name="v_plane", align_bytes=64, offset=KS_GOT_AT)
+        vsc_got = reuse.tile([P, PAGES * DV], U8, name="vsc_got", align_bytes=64, offset=VSC_GOT_AT)
+        nc.vector.tensor_copy(vsc_got[:], vsc_pool[:].indirect(voffs_sb[:]))
         for j in range(PACK):
             nc.sync.dma_start(out=v_plane[j:P:QUAD, :].bitcast(I32), in_=vsc_got[VSC_ROW + j : P : PACK, :].bitcast(I32))
 
-        dealt = vs_pool[:].rearrange("p (u r n h j) -> p r h u n j", u=POOL_PAGES, r=PACK, h=2, j=PACK)
+        turned = psum.tile([P, PACK, P], F32, name="turned", tag="turned")
         for r in range(PACK):
-            for h in range(2):
-                spread = psum.tile([P, PACK, P], F32, name=f"spread{r}_{h}", tag=f"turn{(2 * r + h) % PAGES}")
-                for j in range(PACK):
-                    m = PACK * (PACK * h + j) + r
-                    nc.tensor.transpose(spread[:, j, :], vs_fold[:, m : m + 1].to_broadcast([P, P]), ident[:])
-                nc.scalar.copy(out=dealt[:, r, h], in_=spread[:].rearrange("p j (u n) -> p u n j", u=POOL_PAGES))
+            nc.tensor.transpose(turned[:, r, :], vs_rows[:, r:PAGE:PACK], ident[:])
+        nc.scalar.copy(out=vs_cols[:], in_=turned[:, :, VS_ROW:P].rearrange("s r u -> s u r"))
+        nc.scalar.copy(
+            out=vs_pool[:].rearrange("s (u q r) -> s u q r", u=POOL_PAGES, r=PACK),
+            in_=vs_cols[:].unsqueeze(2).to_broadcast([P, POOL_PAGES, NQ, PACK]),
+        )
 
-        kw_got = [
-            reuse.tile([P, PAGE], U32, name=f"kw_got{e}", align_bytes=64, offset=(e % 2) * PAGE_BYTES)
+        kw_got = [keep.tile([P, PAGE], U32, name=f"kw_got{e}", align_bytes=64) for e in range(PAGES)]
+        kw_part = [
+            reuse.tile([P, PASSES, PAGE], U16, name=f"kw_part{e}", align_bytes=64, offset=PART_AT + e * PART_BYTES)
             for e in range(PAGES)
         ]
-        vw_got = reuse.tile([P, PAGES * DV], U32, name="vw_got", align_bytes=64, offset=PIECE_AT)
-        w_at = {0: 0, 1: PAGE_BYTES}
-        w_f32 = [
-            reuse.tile([P, PAGE], F32, name=f"w_f32{e}", align_bytes=64, offset=w_at[e])
-            if e in w_at
-            else keep.tile([P, PAGE], F32, name=f"w_f32{e}", align_bytes=64)
-            for e in range(PAGES - 1)
-        ]
+        p_sb = [keep.tile([P, PAGE], F32, name=f"p_sb{e}", align_bytes=64) for e in range(PAGES)]
+        w_f32 = [keep.tile([P, PAGE], F32, name=f"w_f32{e}", align_bytes=64) for e in range(PAGES - 1)]
         vs_last = keep.tile([P, PAGE], F32, name="vs_last", align_bytes=64)
-        w_pairs = reuse.tile([P, 2, 2 * P], BF16, name="w_pairs", align_bytes=64, offset=LAST_AT)
-        kw_part = [keep.tile([P, PASSES, PAGE], U16, name=f"kw_part{e}", align_bytes=64) for e in range(PAGES)]
-        p_at = {(PAGES - 1, 0): PIECE_AT}
-        p_sb = {
-            (e, r0): reuse.tile([P, places * P], F32, name=f"p_sb{e}_{r0}", align_bytes=64, offset=p_at[e, r0])
-            if (e, r0) in p_at
-            else keep.tile([P, places * P], F32, name=f"p_sb{e}_{r0}", align_bytes=64)
-            for e, r0, places in PIECES
-        }
-        w_bf = keep.tile([P, PAGES, NQ * PACK], BF16, name="w_bf", align_bytes=64)
+        vw_got = reuse.tile([P, PAGES * DV], U32, name="vw_got", align_bytes=64, offset=PART_AT + PART_BYTES)
+        w_bf = [
+            reuse.tile([P, PAGE], BF16, name=f"w_bf{e}", align_bytes=64, offset=PART_AT + (e + 2) * PART_BYTES)
+            for e in range(PAGES)
+        ]
         w_codes = keep.tile([P, PAGES * NQ], U32, name="w_codes", align_bytes=64)
         w_plane = keep.tile([P, PAGES * NQ], U8, name="w_plane", align_bytes=64)
-        score = [psum.tile([P, PAGE], F32, name=f"score{e}", tag=f"bank{e}") for e in range(PAGES)]
-        w_turn = [psum.tile([P, PACK, P], F32, name=f"w_turn{e}", tag=f"turn{e}") for e in range(PAGES)]
-        y_ps = [psum.tile([P, DV], F32, name=f"y_ps{b}", tag=f"bank{b}") for b in range(B)]
+        score = [psum.tile([P, PACK, NQ], F32, name=f"score{e}", tag=f"bank{e}") for e in range(PAGES)]
+        y_ps = [psum.tile([P, DV], F32, name=f"y_ps{b}", tag=f"result{b}") for b in range(B)]
 
-        def pieces_of(e):
-            return [(r0, places) for page, r0, places in PIECES if page == e]
+        def page_offsets(e):
+            return offs_sb[:, e * PAGE // 16 : (e + 1) * PAGE // 16]
 
         def gather_keys(e):
-            cols = slice(e * PAGE // 16, (e + 1) * PAGE // 16)
-            nc.vector.tensor_copy(kw_got[e][:], kw_pool[:].bitcast(U32).indirect(offs_sb[:, cols]))
+            nc.vector.tensor_copy(kw_got[e][:], kw_pool[:].bitcast(U32).indirect(page_offsets(e)))
 
         def part_keys(e):
-            nc.vector.tensor_copy(kw_part[e][:], kw_got[e][:].bitcast(U16).rearrange("g (n o) -> g o n", o=PASSES))
+            nc.vector.tensor_copy(
+                kw_part[e][:].rearrange("g o (h r s) -> g o h s r", h=2, r=2),
+                kw_got[e][:].bitcast(U16).rearrange("g (s h r o) -> g o h s r", h=2, r=2, o=PASSES),
+            )
 
         def scores(e):
             b = e * PAGE // N
-            order = range(PASSES) if e == 0 else range(PASSES - 1, -1, -1)
-            for o in order:
-                nc.tensor.matmul_mx(
-                    out=score[e][:],
-                    lhsT=qw[b][:, o * NQ : (o + 1) * NQ].bitcast(FP8X4),
-                    lhsT_scale=q_plane[:, (b * PASSES + o) * NQ : (b * PASSES + o + 1) * NQ],
-                    rhs=kw_part[e][:, o, :].bitcast(FP4X4),
-                    rhs_scale=ks_plane[o][:, e * PAGE : (e + 1) * PAGE],
-                    start=(o == order[0]),
-                    stop=(o == order[-1]),
-                )
-            for r0, places in pieces_of(e):
-                nc.scalar.activation(
-                    out=p_sb[e, r0][:].rearrange("q (r s) -> q r s", r=places),
-                    in_=score[e][:].rearrange("q (s r) -> q r s", r=PACK)[:, r0 : r0 + places, :],
-                    func=ACT.Sigmoid,
-                )
+            for r in range(PACK):
+                for o in range(PASSES):
+                    nc.tensor.matmul_mx(
+                        out=score[e][:, r, :],
+                        lhsT=kw_part[e][:, o, r * P : (r + 1) * P].bitcast(FP4X4),
+                        lhsT_scale=ks_plane[:, o, e * PAGE + r * P : e * PAGE + (r + 1) * P],
+                        rhs=qw[b][:, o * NQ : (o + 1) * NQ].bitcast(FP8X4),
+                        rhs_scale=q_plane[:, (b * PASSES + o) * NQ : (b * PASSES + o + 1) * NQ],
+                        start=(o == 0),
+                        stop=(o == PASSES - 1),
+                    )
+            nc.scalar.activation(
+                out=p_sb[e][:].rearrange("s (q r) -> s q r", r=PACK),
+                in_=score[e][:].rearrange("s r q -> s q r"),
+                func=ACT.Sigmoid,
+            )
 
         def weigh(e):
-            for r0, places in pieces_of(e):
-                first, last = r0 * P, (r0 + places) * P
-                cols = slice((e * PAGE + first) // 16, (e * PAGE + last) // 16)
-                nc.vector.tensor_tensor(w_f32[e][:, first:last], vs_pool[:].indirect(offs_sb[:, cols]), p_sb[e, r0][:], MULT)
+            nc.vector.tensor_tensor(w_f32[e][:], vs_pool[:].indirect(page_offsets(e)), p_sb[e][:], MULT)
+            nc.scalar.copy(out=w_bf[e][:], in_=w_f32[e][:])
 
-        def turn(e):
-            for r in range(PACK):
-                nc.tensor.transpose(w_turn[e][:, r, :], w_f32[e][:, r * P : (r + 1) * P], ident[:])
-            nc.scalar.copy(
-                out=w_bf[:, e, :].rearrange("s (q r) -> s q r", r=PACK),
-                in_=w_turn[e][:].rearrange("s r q -> s q r"),
-            )
-
-        def weigh_last():
-            e = PAGES - 1
-            for u, (r0, places) in enumerate(pieces_of(e)):
-                nc.vector.tensor_tensor(
-                    w_pairs[:, u, :].rearrange("q (c i r) -> q c r i", i=PACK, r=places),
-                    p_sb[e, r0][:].rearrange("q (r c i) -> q c r i", i=PACK, r=places),
-                    vs_last[:, r0 * P : (r0 + places) * P].rearrange("q (r c i) -> q c r i", i=PACK, r=places),
-                    MULT,
-                )
-                nc.tensor.transpose(w_turn[e][:, u, :], w_pairs[:, u, :].bitcast(F32), ident[:])
-            nc.scalar.copy(
-                out=w_bf[:, e, :].bitcast(F32).rearrange("s (q u) -> s q u", u=2),
-                in_=w_turn[e][:, 0:2, :].rearrange("s u q -> s q u"),
-            )
-
-        def quantise(first, last):
-            cols = slice(first * NQ, (last + 1) * NQ)
+        def quantise(e):
+            cols = slice(e * NQ, (e + 1) * NQ)
             nc.vector.quantize_mx(
                 out=w_codes[:, cols].bitcast(FP8X4),
                 scales=w_plane[:, cols],
-                in_=w_bf[:, first : last + 1, :].rearrange("s e c -> s (e c)"),
+                in_=w_bf[e][:],
             )
 
-        def mix(e):
-            b, page_in_b = divmod(e, N // PAGE)
+        def mix(e, start, stop):
+            b = e * PAGE // N
             v_cols = slice(e * DV, (e + 1) * DV)
             nc.tensor.matmul_mx(
                 out=y_ps[b][:],
@@ -231,8 +206,8 @@ def tile_attend_pkv4q_sigm_kernel(
                 lhsT_scale=w_plane[:, e * NQ : (e + 1) * NQ],
                 rhs=vw_got[:, v_cols].bitcast(FP8X4),
                 rhs_scale=v_plane[:, v_cols],
-                start=(page_in_b == 0),
-                stop=(page_in_b == N // PAGE - 1),
+                start=start,
+                stop=stop,
             )
 
         def store(b):
@@ -243,24 +218,25 @@ def tile_attend_pkv4q_sigm_kernel(
                 nc.vector.tensor_scalar_mul(y_sb[:], y_ps[b][:], 1.0 / 16.0)
             nc.sync.dma_start(out=out[b], in_=y_sb[:])
 
-        nc.scalar.activation(vs_last[:], vs_pool[:].indirect(offs_sb[:, (PAGES - 1) * PAGE // 16 :]), ACT.Copy)
-        for pair in range(0, PAGES, 2):
-            gather_keys(pair)
-            gather_keys(pair + 1)
-            part_keys(pair)
-            part_keys(pair + 1)
+        nc.scalar.activation(vs_last[:], vs_pool[:].indirect(page_offsets(PAGES - 1)), ACT.Copy)
+        gather_keys(0)
+        for e in range(PAGES):
+            if e + 1 < PAGES:
+                gather_keys(e + 1)
+            part_keys(e)
         for e in range(PAGES):
             scores(e)
         for e in range(PAGES - 1):
             weigh(e)
-            turn(e)
-        weigh_last()
-        quantise(0, 1)
         nc.vector.tensor_copy(vw_got[:], vw_pool[:].bitcast(U32).indirect(voffs_sb[:]))
-        mix(0)
-        mix(1)
+        nc.vector.tensor_tensor(w_bf[PAGES - 1][:], p_sb[PAGES - 1][:], vs_last[:], MULT)
+        quantise(0)
+        quantise(1)
+        mix(0, True, False)
+        mix(1, False, True)
         store(0)
-        for e in (PAGES - 2, PAGES - 1):
-            quantise(e, e)
-            mix(e)
+        quantise(3)
+        mix(3, True, False)
+        quantise(2)
+        mix(2, False, True)
         store(1)

@@ -61,17 +61,14 @@ def tile_attend_pkv4q_sigm_kernel(
         vsc_pool = keep.tile([P, POOL_PAGES * DV], U8, name="vsc_pool", align_bytes=64)
         v_plane = keep.tile([P, PAGES * DV], U8, name="v_plane", align_bytes=64)
         qw_first = keep.tile([P, PASSES * NQ], I32, name="qw_first", align_bytes=64)
-        qs_rows = keep.tile([PACK, B * PASSES, QUADS, NQ // 4], I32, name="qs_rows", align_bytes=64)
+        ks_plane = keep.tile([P, PASSES, B * N], U8, name="ks_plane", align_bytes=64)
         q_plane = keep.tile([P, B * PASSES * NQ], U8, name="q_plane", align_bytes=64)
         ident = keep.tile([P, P], F32, name="ident")
 
+        nc.gpsimd.memset(q_plane[:].bitcast(I32), 0)
         nc.sync.dma_start(out=ks_pool[KS_ROW:P, :].bitcast(I32), in_=k_scales.rearrange("o f t -> f o t").bitcast(I32))
-        nc.scalar.dma_start(
-            out=qs_rows[:].rearrange("j c u x -> j (c u) x"),
-            in_=q_scales.rearrange("b o (u j) q -> j (b o u) q", j=PACK).bitcast(I32),
-        )
-        nc.sync.dma_start(offs_sb[:], offs)
         nc.scalar.dma_start(out=vs_rows[VS_ROW:P, :], in_=vs[0:1].rearrange("a (u m) -> (a u) m", m=PAGE))
+        nc.sync.dma_start(offs_sb[:], offs)
         nc.sync.dma_start(voffs_sb[:], voffs)
         nc.scalar.dma_start(
             out=vsc_pool[VSC_ROW:P, :].bitcast(I32).rearrange("f (u x) -> f u x", u=POOL_PAGES),
@@ -85,20 +82,21 @@ def tile_attend_pkv4q_sigm_kernel(
                 in_=q_words[b].rearrange("o g q r -> g o (q r)").bitcast(I32),
             )
 
-        load_queries(0, qw_first)
-
-        nc.gpsimd.memset(vs_rows[0:VS_ROW, :], 0.0)
-        make_identity(nc, ident[:])
-        nc.gpsimd.memset(v_plane[:].bitcast(I32), 0)
-        nc.vector.memset(q_plane[:].bitcast(I32), 0)
+        nc.vector.memset(vs_rows[0:VS_ROW, :], 0.0)
         nc.vector.memset(ks_pool[0:KS_ROW, :].bitcast(I32), 0)
         nc.vector.memset(vsc_pool[0:VSC_ROW, :].bitcast(I32), 0)
+        make_identity(nc, ident[:])
+        for o in range(PASSES):
+            nc.gpsimd.memset(ks_plane[:, o, :].bitcast(I32), 0)
+        nc.gpsimd.memset(v_plane[:].bitcast(I32), 0)
 
+        qs_rows = q_scales.rearrange("b o f q -> f (b o) q").bitcast(I32)
         for quad in range(QUADS):
-            nc.vector.tensor_copy(
-                q_plane[QUAD * quad : QUAD * quad + PACK, :].bitcast(I32).rearrange("j (c x) -> j c x", c=B * PASSES),
-                qs_rows[:, :, quad, :],
+            nc.sync.dma_start(
+                out=q_plane[QUAD * quad : QUAD * quad + PACK, :].bitcast(I32).rearrange("j (c x) -> j c x", c=B * PASSES),
+                in_=qs_rows[PACK * quad : PACK * (quad + 1)],
             )
+        load_queries(0, qw_first)
 
         for b in range(B):
             nc.vector.tensor_copy(ks_got[b][:], ks_pool[:].indirect(offs_sb[:, b * N // 16 : (b + 1) * N // 16]))
@@ -107,7 +105,6 @@ def tile_attend_pkv4q_sigm_kernel(
                 ks_dealt[:, b * N : (b + 1) * N].rearrange("f (e h r s) -> f e h s r", e=N // PAGE, h=2, r=2),
                 ks_got[b][:].rearrange("f (e s h r) -> f e h s r", e=N // PAGE, h=2, r=2),
             )
-        ks_plane = reuse.tile([P, PASSES, B * N], U8, name="ks_plane", align_bytes=64, offset=KS_AT)
         for quad in (0, 2, 1, 3):
             first = KS_ROW + PASSES * PACK * quad
             nc.sync.dma_start(

from contextlib import ExitStack

import concourse.mybir as mybir
from concourse.masks import make_identity

B, N, T, D, DV, NQ = 2, 1024, 4096, 1024, 128, 128
P = 128
PAGE = 512
PACK = 4
PAGES = B * N // PAGE
POOL_PAGES = T // PAGE
PASSES = D // 512
SCALE_ROWS = 16
QUAD = 32
QUADS = P // QUAD
KS_ROW = P - PASSES * SCALE_ROWS
VSC_ROW = P - SCALE_ROWS
VS_ROW = P - POOL_PAGES
FLOPS = 2 * B * NQ * N * (D + DV)

KS_AT = 0
KS_GOT_AT = KS_AT + T
VSC_GOT_AT = KS_GOT_AT
QW_LATE_AT = VSC_GOT_AT + PAGES * DV
VW_AT = QW_LATE_AT + 4 * PASSES * NQ
PART_AT = VW_AT + 4 * POOL_PAGES * DV
PART_BYTES = 2 * PASSES * PAGE

F32 = mybir.dt.float32
BF16 = mybir.dt.bfloat16
I32 = mybir.dt.int32
U32 = mybir.dt.uint32
U16 = mybir.dt.uint16
U8 = mybir.dt.uint8
FP8X4 = mybir.dt.float8_e4m3fn_x4
FP4X4 = mybir.dt.float4_e2m1fn_x4
ACT = mybir.ActivationFunctionType
MULT = mybir.AluOpType.mult


def tile_attend_pkv4q_sigm_kernel(
    tc, q_words, q_scales, k_words, k_scales, v_words, v_scales, vs, offs, voffs, out
):
    nc = tc.nc
    with ExitStack() as ctx:
        keep = ctx.enter_context(tc.tile_pool(name="keep", bufs=1))
        reuse = ctx.enter_context(tc.tile_pool(name="reuse", bufs=1))
        psum = ctx.enter_context(tc.psum_pool(name="psum", bufs=1))

        offs_sb = keep.tile([P, B * N // 16], U16, name="offs_sb")
        voffs_sb = keep.tile([P, PAGES * DV // 16], U16, name="voffs_sb")
        kw_pool = keep.tile([P, T], I32, name="kw_pool", align_bytes=64)
        ks_pool = reuse.tile([P, T], U8, name="ks_pool", align_bytes=64, offset=KS_AT)
        ks_got = [
            reuse.tile([P, N], U8, name=f"ks_got{b}", align_bytes=64, offset=KS_GOT_AT + b * N) for b in range(B)
        ]
        ks_dealt = keep.tile([P, B * N], U8, name="ks_dealt", align_bytes=64)
        vs_rows = keep.tile([P, PAGE], F32, name="vs_rows", align_bytes=64)
        vs_cols = keep.tile([P, POOL_PAGES, PACK], F32, name="vs_cols", align_bytes=64)
        vs_pool = keep.tile([P, T], F32, name="vs_pool", align_bytes=64)
        vsc_pool = keep.tile([P, POOL_PAGES * DV], U8, name="vsc_pool", align_bytes=64)
        v_plane = keep.tile([P, PAGES * DV], U8, name="v_plane", align_bytes=64)
        qw_first = keep.tile([P, PASSES * NQ], I32, name="qw_first", align_bytes=64)
        ks_plane = keep.tile([P, PASSES, B * N], U8, name="ks_plane", align_bytes=64)
        q_plane = keep.tile([P, B * PASSES * NQ], U8, name="q_plane", align_bytes=64)
        ident = keep.tile([P, P], F32, name="ident")

        nc.gpsimd.memset(q_plane[:].bitcast(I32), 0)
        nc.sync.dma_start(out=ks_pool[KS_ROW:P, :].bitcast(I32), in_=k_scales.rearrange("o f t -> f o t").bitcast(I32))
        nc.scalar.dma_start(out=vs_rows[VS_ROW:P, :], in_=vs[0:1].rearrange("a (u m) -> (a u) m", m=PAGE))
        nc.sync.dma_start(offs_sb[:], offs)
        nc.sync.dma_start(voffs_sb[:], voffs)
        nc.scalar.dma_start(
            out=vsc_pool[VSC_ROW:P, :].bitcast(I32).rearrange("f (u x) -> f u x", u=POOL_PAGES),
            in_=v_scales.rearrange("u f e -> f u e").bitcast(I32),
        )
        nc.sync.dma_start(out=kw_pool[:], in_=k_words[0].rearrange("g t r -> g (t r)").bitcast(I32))

        def load_queries(b, tile):
            nc.sync.dma_start(
                out=tile[:].rearrange("g (o q) -> g o q", q=NQ),
                in_=q_words[b].rearrange("o g q r -> g o (q r)").bitcast(I32),
            )

        nc.vector.memset(vs_rows[0:VS_ROW, :], 0.0)
        nc.vector.memset(ks_pool[0:KS_ROW, :].bitcast(I32), 0)
        nc.vector.memset(vsc_pool[0:VSC_ROW, :].bitcast(I32), 0)
        make_identity(nc, ident[:])
        for o in range(PASSES):
            nc.gpsimd.memset(ks_plane[:, o, :].bitcast(I32), 0)
        nc.gpsimd.memset(v_plane[:].bitcast(I32), 0)

        qs_rows = q_scales.rearrange("b o f q -> f (b o) q").bitcast(I32)
        for quad in range(QUADS):
            nc.sync.dma_start(
                out=q_plane[QUAD * quad : QUAD * quad + PACK, :].bitcast(I32).rearrange("j (c x) -> j c x", c=B * PASSES),
                in_=qs_rows[PACK * quad : PACK * (quad + 1)],
            )
        load_queries(0, qw_first)

        for b in range(B):
            nc.vector.tensor_copy(ks_got[b][:], ks_pool[:].indirect(offs_sb[:, b * N // 16 : (b + 1) * N // 16]))
        for b in range(B):
            nc.vector.tensor_copy(
                ks_dealt[:, b * N : (b + 1) * N].rearrange("f (e h r s) -> f e h s r", e=N // PAGE, h=2, r=2),
                ks_got[b][:].rearrange("f (e s h r) -> f e h s r", e=N // PAGE, h=2, r=2),
            )
        for quad in (0, 2, 1, 3):
            first = KS_ROW + PASSES * PACK * quad
            nc.sync.dma_start(
                out=ks_plane[QUAD * quad : QUAD * quad + PACK].bitcast(I32),
                in_=ks_dealt[first : first + PASSES * PACK, :].bitcast(I32),
            )
        qw_late = reuse.tile([P, PASSES * NQ], I32, name="qw_late", align_bytes=64, offset=QW_LATE_AT)
        load_queries(1, qw_late)
        qw = [qw_first, qw_late]
        vw_pool = reuse.tile([P, POOL_PAGES * DV], I32, name="vw_pool", align_bytes=64, offset=VW_AT)
        nc.sync.dma_start(
            out=vw_pool[:].rearrange("g (u e) -> g u e", e=DV),
            in_=v_words.rearrange("u g e r -> g u (e r)").bitcast(I32),
        )
        vsc_got = reuse.tile([P, PAGES * DV], U8, name="vsc_got", align_bytes=64, offset=VSC_GOT_AT)
        nc.vector.tensor_copy(vsc_got[:], vsc_pool[:].indirect(voffs_sb[:]))
        for j in range(PACK):
            nc.sync.dma_start(out=v_plane[j:P:QUAD, :].bitcast(I32), in_=vsc_got[VSC_ROW + j : P : PACK, :].bitcast(I32))

        turned = psum.tile([P, PACK, P], F32, name="turned", tag="turned")
        for r in range(PACK):
            nc.tensor.transpose(turned[:, r, :], vs_rows[:, r:PAGE:PACK], ident[:])
        nc.scalar.copy(out=vs_cols[:], in_=turned[:, :, VS_ROW:P].rearrange("s r u -> s u r"))
        nc.scalar.copy(
            out=vs_pool[:].rearrange("s (u q r) -> s u q r", u=POOL_PAGES, r=PACK),
            in_=vs_cols[:].unsqueeze(2).to_broadcast([P, POOL_PAGES, NQ, PACK]),
        )

        kw_got = [keep.tile([P, PAGE], U32, name=f"kw_got{e}", align_bytes=64) for e in range(PAGES)]
        kw_part = [
            reuse.tile([P, PASSES, PAGE], U16, name=f"kw_part{e}", align_bytes=64, offset=PART_AT + e * PART_BYTES)
            for e in range(PAGES)
        ]
        p_sb = [keep.tile([P, PAGE], F32, name=f"p_sb{e}", align_bytes=64) for e in range(PAGES)]
        w_f32 = [keep.tile([P, PAGE], F32, name=f"w_f32{e}", align_bytes=64) for e in range(PAGES - 1)]
        vs_last = keep.tile([P, PAGE], F32, name="vs_last", align_bytes=64)
        vw_got = reuse.tile([P, PAGES * DV], U32, name="vw_got", align_bytes=64, offset=PART_AT + PART_BYTES)
        w_bf = [
            reuse.tile([P, PAGE], BF16, name=f"w_bf{e}", align_bytes=64, offset=PART_AT + (e + 2) * PART_BYTES)
            for e in range(PAGES)
        ]
        w_codes = keep.tile([P, PAGES * NQ], U32, name="w_codes", align_bytes=64)
        w_plane = keep.tile([P, PAGES * NQ], U8, name="w_plane", align_bytes=64)
        score = [psum.tile([P, PACK, NQ], F32, name=f"score{e}", tag=f"bank{e}") for e in range(PAGES)]
        y_ps = [psum.tile([P, DV], F32, name=f"y_ps{b}", tag=f"result{b}") for b in range(B)]

        def page_offsets(e):
            return offs_sb[:, e * PAGE // 16 : (e + 1) * PAGE // 16]

        def gather_keys(e):
            nc.vector.tensor_copy(kw_got[e][:], kw_pool[:].bitcast(U32).indirect(page_offsets(e)))

        def part_keys(e):
            nc.vector.tensor_copy(
                kw_part[e][:].rearrange("g o (h r s) -> g o h s r", h=2, r=2),
                kw_got[e][:].bitcast(U16).rearrange("g (s h r o) -> g o h s r", h=2, r=2, o=PASSES),
            )

        def scores(e):
            b = e * PAGE // N
            for r in range(PACK):
                for o in range(PASSES):
                    nc.tensor.matmul_mx(
                        out=score[e][:, r, :],
                        lhsT=kw_part[e][:, o, r * P : (r + 1) * P].bitcast(FP4X4),
                        lhsT_scale=ks_plane[:, o, e * PAGE + r * P : e * PAGE + (r + 1) * P],
                        rhs=qw[b][:, o * NQ : (o + 1) * NQ].bitcast(FP8X4),
                        rhs_scale=q_plane[:, (b * PASSES + o) * NQ : (b * PASSES + o + 1) * NQ],
                        start=(o == 0),
                        stop=(o == PASSES - 1),
                    )
            nc.scalar.activation(
                out=p_sb[e][:].rearrange("s (q r) -> s q r", r=PACK),
                in_=score[e][:].rearrange("s r q -> s q r"),
                func=ACT.Sigmoid,
            )

        def weigh(e):
            nc.vector.tensor_tensor(w_f32[e][:], vs_pool[:].indirect(page_offsets(e)), p_sb[e][:], MULT)
            nc.scalar.copy(out=w_bf[e][:], in_=w_f32[e][:])

        def quantise(e):
            cols = slice(e * NQ, (e + 1) * NQ)
            nc.vector.quantize_mx(
                out=w_codes[:, cols].bitcast(FP8X4),
                scales=w_plane[:, cols],
                in_=w_bf[e][:],
            )

        def mix(e, start, stop):
            b = e * PAGE // N
            v_cols = slice(e * DV, (e + 1) * DV)
            nc.tensor.matmul_mx(
                out=y_ps[b][:],
                lhsT=w_codes[:, e * NQ : (e + 1) * NQ].bitcast(FP8X4),
                lhsT_scale=w_plane[:, e * NQ : (e + 1) * NQ],
                rhs=vw_got[:, v_cols].bitcast(FP8X4),
                rhs_scale=v_plane[:, v_cols],
                start=start,
                stop=stop,
            )

        def store(b):
            y_sb = keep.tile([P, DV], F32, name=f"y_sb{b}")
            if b == 0:
                nc.scalar.activation(out=y_sb[:], in_=y_ps[b][:], func=ACT.Copy, scale=1.0 / 16.0)
            else:
                nc.vector.tensor_scalar_mul(y_sb[:], y_ps[b][:], 1.0 / 16.0)
            nc.sync.dma_start(out=out[b], in_=y_sb[:])

        nc.scalar.activation(vs_last[:], vs_pool[:].indirect(page_offsets(PAGES - 1)), ACT.Copy)
        gather_keys(0)
        for e in range(PAGES):
            if e + 1 < PAGES:
                gather_keys(e + 1)
            part_keys(e)
        for e in range(PAGES):
            scores(e)
        for e in range(PAGES - 1):
            weigh(e)
        nc.vector.tensor_copy(vw_got[:], vw_pool[:].bitcast(U32).indirect(voffs_sb[:]))
        nc.vector.tensor_tensor(w_bf[PAGES - 1][:], p_sb[PAGES - 1][:], vs_last[:], MULT)
        quantise(0)
        quantise(1)
        mix(0, True, False)
        mix(1, False, True)
        store(0)
        quantise(3)
        mix(3, True, False)
        quantise(2)
        mix(2, False, True)
        store(1)
